import numpy as np, ml_dtypes
CORES = [2,3,42,43,82,83,122,123]
N = 8
import mx_ref
BF = ml_dtypes.bfloat16
def cols(t, e):
    v = np.concatenate([t.reshape(128, -1, 4), np.zeros((128, 1, 4), BF)], axis=1)
    return np.ascontiguousarray(v[:, e]).reshape(128, -1)
def cut(t, i, w=512):
    return t[:, w * i:w * i + w]
def f(rng, *shape):
    return mx_ref.flush((rng.standard_normal(shape, dtype=np.float32) * np.exp2(rng.integers(-2, 3, shape[:-1] + (1,)))).astype(BF))
def wide(rng, *shape, cols=0):
    v = rng.standard_normal(shape, dtype=np.float32) * np.exp2(rng.integers(-12, 13, shape)).astype(np.float32)
    if cols: v *= np.repeat(np.exp2(rng.integers(-cols, cols + 1, shape[:-2] + (1, shape[-1] // 4))) * (rng.random(shape[:-2] + (1, shape[-1] // 4)) > 0.0625), 4, axis=-1).astype(np.float32)
    return mx_ref.flush(v.astype(BF))
P, K, R, O = 256, 96, 4, 3
PART = [1, 2, 4, 1]
def scores(c, qt):
    k = mx_ref.quantize(np.concatenate([qt[r][:, :4 * R] for r in range(N)], axis=1))
    s = [mx_ref.matmul(mx_ref.quantize(cut(c[q], i)), k) for q in range(N) for i in range(P // 128)]
    return np.concatenate(s).reshape(N * P, N, R)
def play(s):
    held, use, out = np.arange(N * P).reshape(N, P), np.zeros((N, P), np.float32), []
    for t in range(R):
        left = []
        for r in range(N):
            v = s[held[r], r, t]
            use[r] = use[r] + v * v
            left.append(np.argsort(use[r], kind="stable")[:K])
        new = held.copy()
        for r in range(N):
            p = r ^ PART[t]
            new[r, left[r]] = held[p, left[p]]
            use[r, left[r]] = 0
        held = new
        out.append(held)
    return np.stack(out)
def fit(s):
    a = np.abs(s)
    return bool(np.isfinite(a).all() and ((a == 0) | (a >= 2.0 ** -60) & (a <= 2.0 ** 60)).all())
def times(t, v):
    return mx_ref.flush((t.astype(np.float32) * np.asarray(v, np.float32)).astype(BF))
def plain(rng):
    q = np.array(f(rng, N, 128, 512))
    q[:, :, 4 * R:] = 0
    return {"c": f(rng, N, 128, 4 * P), "qt": q, "w": f(rng, N, 128, 512 * O)}
def first(make, good=None):
    for i in range(50):
        d = make()
        s = scores(d["c"], d["qt"])
        if fit(s) and (good is None or good(s)): return d
    raise RuntimeError("no draw of 50 is fit")
def athome(s):
    h, a = play(s), np.ones((N, R + 1, P), bool)
    for r in range(N):
        for t in range(R): a[r, t + 1] = np.isin(np.arange(P * r, P * r + P), h[t, r])
    return a
def setup_inputs(rng):
    return first(lambda: plain(rng))
def setup_inputs_sides(rng):
    top = np.arange(128) < 64
    def make():
        d = plain(rng)
        half = np.stack([rng.permutation(P) < P // 2 for r in range(N)])
        d["c"] = times(d["c"], np.repeat(half[:, None, :] == top[None, :, None], 4, axis=2))
        for t in range(R):
            g = np.where(top == (PART[t] == 1), 1.0, 2.0 ** -6) * 4.0 ** t
            d["qt"][:, :, 4 * t:4 * t + 4] = times(d["qt"][:, :, 4 * t:4 * t + 4], g[None, :, None])
        return d
    def good(s):
        a = athome(s)
        return bool((~a[:, :-1] & a[:, 1:]).any(axis=(1, 2)).all())
    return first(make, good)
def setup_inputs_ties(rng):
    def make():
        d = plain(rng)
        d["c"] = np.stack([times(cols(d["c"][r], rng.integers(0, 6, P)), np.repeat(1 - 2 * rng.integers(0, 2, P), 4)) for r in range(N)])
        return d
    def good(s):
        for r in range(N):
            v = s[P * r:P * r + P, r, 0]
            u = np.sort(v * v)
            if u[K - 1] != u[K]: return False
        return True
    return first(make, good)
def setup_inputs_shrink(rng):
    low = np.arange(N) >= N - N // 4
    def make():
        d = plain(rng)
        size = np.exp2(np.where(low, -30.0, 23.0)[:, None] + 2 * rng.random((N, P))) * (1 - 2 * rng.integers(0, 2, (N, P)))
        d["c"] = ((1 + rng.random((N, 128, 4 * P))) * np.repeat(size, 4, axis=1)[:, None, :]).astype(np.float32).astype(BF)
        on = ~low[:, None] | np.stack([rng.permutation(128) < 2 for r in range(N)])
        for t in range(R):
            g = np.exp2(np.where(low, 8.0 * (R - 1 - t) - 30.0, 21.0 - 8.0 * t))
            d["qt"][:, :, 4 * t:4 * t + 4] = ((1 + rng.random((N, 128, 4))) * (g[:, None] * on)[:, :, None]).astype(np.float32).astype(BF)
        return d
    def good(s):
        h, a, b = play(s), np.zeros(N, bool), np.zeros(N, bool)
        for r in range(N):
            at, use, since = np.arange(P * r, P * r + P), np.zeros(P, np.float32), np.zeros(P, int)
            if low[r] and np.abs(s[at, r, R - 1]).max() > 2.0 ** -50 or not low[r] and np.abs(s[at, r, 0]).min() < 2.0 ** 50: return False
            for t in range(R):
                v = s[at, r]
                use = use + v[:, t] * v[:, t]
                sums = np.concatenate([np.zeros((P, 1), np.float32), np.cumsum(v * v, axis=1)], axis=1)
                diff = sums[:, t + 1] - sums[np.arange(P), since]
                a[r] |= (np.argsort(use, kind="stable")[:K] != np.argsort(diff, kind="stable")[:K]).any()
                b[r] |= np.sort(use)[K - 1] > 1e30
                moved = h[t, r] != at
                at = h[t, r]
                use[moved] = 0
                since[moved] = t + 1
        return bool(2 * a.sum() > N and 2 * b.sum() > N)
    return first(make, good)
def setup_inputs_turn(rng):
    on = (np.arange(128) // (128 // N))[None, :] == np.arange(N)[:, None]
    def make():
        d = plain(rng)
        d["c"] = times(d["c"], np.where(on, 2.0 ** -8, 1.0)[:, :, None])
        d["qt"] = times(d["qt"], on[:, :, None])
        return d
    return first(make, lambda s: bool((~athome(s)).any(axis=1).all()))
def setup_inputs_spread(rng):
    return first(lambda: {**plain(rng), "c": wide(rng, N, 128, 4 * P, cols=6)})
def check_inputs(d):
    b = []
    for k in ("c", "qt", "w"):
        v = np.abs(d[k].astype(np.float32))
        if not (np.isfinite(v).all() and ((v == 0) | (v >= 2.0 ** -30) & (v <= 2.0 ** 30)).all()): b.append("a value of " + k)
    if (d["qt"][:, :, 4 * R:].astype(np.float32) != 0).any(): b.append("qt has numbers behind its first R columns")
    if not b and not fit(scores(d["c"], d["qt"])): b.append("a score")
    return b
def reference(c, qt, w):
    held = play(scores(c, qt))
    every = np.concatenate([c[q] for q in range(N)], axis=1)
    y = np.zeros((N, 128, R * O * P), np.float32)
    for r in range(N):
        u, at = np.unique(held[:, r].reshape(-1), return_inverse=True)
        at = at.reshape(R, P)
        q = mx_ref.quantize(cols(every, np.concatenate([u, np.full(-len(u) % 4, -1)])))
        for o in range(O):
            z = mx_ref.matmul(mx_ref.quantize(cut(w[r], o)), q)
            for t in range(R):
                i = (t * O + o) * P
                y[r, :, i:i + P] = z[:, at[t]]
    return {"y": y}

@@ -1,0 +1,390 @@
+from concourse.mybir import dt, AluOpType as A, ActivationFunctionType as AF
+
+P, K, R, O = 256, 96, 4, 3
+PART = [1, 2, 4, 1]
+NS = [P + K * t for t in range(R + 1)]
+EPS = 2.0 ** -125
+
+SCRATCH = {"cb": ("sbuf", [128, 4 * P], "bfloat16"), "qb": ("sbuf", [128, 512], "bfloat16"), "wb": ("sbuf", [128, 512 * O], "bfloat16")}
+SEMAPHORES = ["sg", "sv", "ss", "st", "al", "ll"] + ["d%d" % i for i in range(48)]
+for _b, _n in (("q", 128), ("qr", 128 * R), ("wt", 128 * O), ("w4", 128), ("h", P), ("out1", K), ("out2", K), ("out3", K)):
+    SCRATCH[_b + "c"] = ("sbuf", [128, _n], "float8_e4m3fn_x4")
+    SCRATCH[_b + "s"] = ("sbuf", [128, _n], "uint8")
+for _t in range(R):
+    SCRATCH["w%dc" % _t] = ("sbuf", [128, NS[_t]], "float8_e4m3fn_x4")
+    SCRATCH["w%ds" % _t] = ("sbuf", [128, NS[_t]], "uint8")
+    SCRATCH["yb%d" % _t] = ("sbuf", [128, O * P], "float32")
+    SCRATCH["cw%d" % _t] = ("sbuf", [128, 272], "float32")
+    SCRATCH["fy%d" % _t] = ("sbuf", [128, 16], "uint16")
+    SCRATCH["win%d" % _t] = ("sbuf", [128, 272], "bfloat16" if _t < 3 else "float32")
+    SCRATCH["lst%d" % _t] = ("sbuf", [128, 16], "uint16")
+    SEMAPHORES += ["ac%d" % _t, "as%d" % _t, "lc%d" % _t, "ls%d" % _t]
+for _t in range(R + 1):
+    SCRATCH["srow%d" % _t] = ("sbuf", [128, 160], "bfloat16" if _t < 3 else "float32")
+for _o in range(O):
+    SCRATCH["yp%d" % _o] = ("sbuf", [128, NS[4]], "float32")
+for _b in range(8):
+    SCRATCH["ps%d" % _b] = ("psum", [128, 512], "float32")
+for _b, _n in (("wr", NS[3]), ("wc", NS[3]), ("sq", 512), ("hq", P), ("u64", 64), ("t4", 64), ("rr", P), ("mm", P), ("pr", P), ("p2", 8), ("iot", P),
+               ("ttf", 224), ("tsf", 288), ("a7", 8), ("s8", 8), ("cz", 96), ("ctr", 96)):
+    SCRATCH[_b] = ("sbuf", [128, _n], "float32")
+for _b, _n in (("ttb", 224), ("tsb", 288), ("c0", P), ("c1", P), ("kk", P), ("r8", 8)):
+    SCRATCH[_b] = ("sbuf", [128, _n], "bfloat16")
+for _b, _n in (("qoff", 8 * R), ("off", 8), ("hl", 8), ("co", 8), ("fl", 16), ("alst", 8)):
+    SCRATCH[_b] = ("sbuf", [128, _n], "uint16")
+
+
+def rank_program(g, core, T, topo):
+    rank = T.rank_of(core)
+    if rank is None:
+        return
+    Q = {"g": g, "v": g.vector, "s": g.scalar, "t": g.tensor, "y": g.sync}
+    own = {"g": "sg", "v": "sv", "s": "ss", "t": "st"}
+    count = {}
+    waited = {q: {} for q in Q}
+    recs = {}
+    ndma = [0]
+
+    def rg(b, c0, c1, p0=0, p1=128, lane=None):
+        return (b, c0, c1, p0, p1, lane)
+
+    def meets(a, b):
+        if a[0][:2] == "ps":
+            return True
+        if a[5] is not None and b[5] is not None and a[5] != b[5]:
+            return False
+        return a[1] < b[2] and b[1] < a[2] and a[3] < b[4] and b[3] < a[4]
+
+    def covers(a, b):
+        return a[0][:2] == "ps" or (a[5] is None and a[1] <= b[1] and a[2] >= b[2] and a[3] <= b[3] and a[4] >= b[4])
+
+    def need(q, reads, writes):
+        w = {}
+        for regs, wr in ((reads, False), (writes, True)):
+            for r in regs:
+                for (x, xq, sem, n, xw) in recs.get(r[0], []):
+                    if not (wr or xw) or not meets(r, x):
+                        continue
+                    if wr and not xw and xq == q and q != "y":
+                        continue
+                    if r[0][:2] == "ps" and xq == q:
+                        continue
+                    w[sem] = max(w.get(sem, 0), n)
+        for sem in w:
+            if waited[q].get(sem, 0) < w[sem]:
+                Q[q].wait_ge(T.sem[sem], w[sem])
+                waited[q][sem] = w[sem]
+
+    def note(q, sem, n, reads, writes):
+        for r in writes:
+            recs[r[0]] = [e for e in recs.get(r[0], []) if not covers(r, e[0])]
+        for r in writes:
+            recs.setdefault(r[0], []).append((r, q, sem, n, True))
+        for r in reads:
+            recs.setdefault(r[0], []).append((r, q, sem, n, False))
+
+    def do(q, call, reads, writes):
+        need(q, reads, writes)
+        if q == "g" and count.get("sg", 0) > waited["g"].get("sg", 0):
+            g.wait_ge(T.sem.sg, count["sg"])
+            waited["g"]["sg"] = count["sg"]
+        ins = call()
+        sem = own[q]
+        count[sem] = count.get(sem, 0) + 1
+        ins.then_inc(T.sem[sem], 1)
+        note(q, sem, count[sem], reads, writes)
+
+    def dma(q, out, in_, reads, writes):
+        need(q, reads, writes)
+        sem = "d%d" % ndma[0]
+        ndma[0] += 1
+        Q[q].dma_start(out, in_).then_inc(T.sem[sem], 16)
+        count[sem] = 16
+        note("y" if q == "y" else q + "d", sem, 16, reads, writes)
+
+    def send(t, out, in_, reads, writes, sa, sl):
+        dst = T.cores[rank ^ PART[t]]
+        rid, pid, _ = topo.addr(dst)
+        need("g", reads, [])
+        g.remote_dma(out, in_, T.sem[sa], T.sem[sl], pid, rid, topo.mask(core, dst))
+        count[sl] = len(topo.engines(core, dst))
+        count[sa] = len(topo.engines(dst, core))
+        note("r", sa, count[sa], [], writes)
+
+    def send_codes(t, ob, o0, ib, n):
+        for k in ("c", "s"):
+            i, o = T[ib + k][:, 0:n], T[ob + k][:, o0:o0 + n]
+            if k == "c":
+                i, o = i.bitcast(dt.uint8), o.bitcast(dt.uint8)
+            send(t, o, i, [rg(ib + k, 0, n)], [rg(ob + k, o0, o0 + n)], "a%s%d" % (k, t), "l%s%d" % (k, t))
+
+    def cp(q, ob, oc, ib, ic, p=(0, 128), ip=None):
+        ip = ip or p
+        o = T[ob][p[0]:p[1], slice(*oc)]
+        i = T[ib][ip[0]:ip[1], slice(*ic)]
+        rd = [rg(ib, ic[0], ic[1], ip[0], ip[1])]
+        wr = [rg(ob, oc[0], oc[1], p[0], p[1], (oc[0] % oc[2]) if len(oc) > 2 else None)]
+        if q == "v":
+            do("v", lambda: g.vector.tensor_copy(o, i), rd, wr)
+        else:
+            do("s", lambda: g.scalar.activation(o, i, AF.Copy), rd, wr)
+
+    def ts(out, in0, s1, s2, op0, op1, rd, wr):
+        if op1 is None:
+            do("v", lambda: g.vector.tensor_scalar(out, in0, s1, None, op0), rd, wr)
+        else:
+            do("v", lambda: g.vector.tensor_scalar(out, in0, s1, s2, op0, op1), rd, wr)
+
+    def tt(out, a, b, op, rd, wr):
+        do("v", lambda: g.vector.tensor_tensor(out, a, b, op), rd, wr)
+
+    def fill(b, c0, c1, v):
+        do("v", lambda: g.vector.memset(T[b][:, c0:c1], v), [], [rg(b, c0, c1)])
+
+    def tr(ob, o0, ib, i0, n):
+        do("v", lambda: g.vector.transpose(T[ob][:, o0:o0 + n], T[ib][:, i0:i0 + n]), [rg(ib, i0, i0 + n)], [rg(ob, o0, o0 + n)])
+
+    def pick_codes(ob, o0, ib, n, lb, l0, k):
+        c, oc = ib + "c", ob + "c"
+        do("v", lambda: g.vector.tensor_copy(T[oc][:, o0:o0 + k].bitcast(dt.uint32), T[c][:, 0:n].bitcast(dt.uint32).indirect(T[lb][:, l0:l0 + k // 16])),
+           [rg(c, 0, n), rg(lb, l0, l0 + k // 16)], [rg(oc, o0, o0 + k)])
+
+    def pick_scales(ob, o0, ib, n, lb, l0, k):
+        s, os_ = ib + "s", ob + "s"
+        do("s", lambda: g.scalar.activation(T[os_][:, o0:o0 + k], T[s][:, 0:n].indirect(T[lb][:, l0:l0 + k // 16]), AF.Copy),
+           [rg(s, 0, n), rg(lb, l0, l0 + k // 16)], [rg(os_, o0, o0 + k)])
+
+    def mm(bank, lc, l0, rc, r0, n):
+        lh, ls, rh, rs = T[lc + "c"], T[lc + "s"], T[rc + "c"], T[rc + "s"]
+        do("t", lambda: g.tensor.matmul_mx(T[bank][:, 0:n], lh[:, l0:l0 + 128], ls[:, l0:l0 + 128], rh[:, r0:r0 + n], rs[:, r0:r0 + n], True, True),
+           [rg(lc + "c", l0, l0 + 128), rg(lc + "s", l0, l0 + 128), rg(rc + "c", r0, r0 + n), rg(rc + "s", r0, r0 + n)], [rg(bank, 0, 512)])
+
+    def quantize(ob, o0, n, ib):
+        c, s = T[ob + "c"], T[ob + "s"]
+        do("v", lambda: g.vector.quantize_mx(c[:, o0:o0 + n], s[:, o0:o0 + n], T[ib][:, 4 * o0:4 * (o0 + n)]),
+           [rg(ib, 4 * o0, 4 * (o0 + n))], [rg(ob + "c", o0, o0 + n), rg(ob + "s", o0, o0 + n)])
+
+    def square(ob, o0, bank, i0, n):
+        do("s", lambda: g.scalar.activation(T[ob][:, o0:o0 + n], T[bank][:, i0:i0 + n], AF.Square), [rg(bank, 0, 512)], [rg(ob, o0, o0 + n)])
+
+    def lift(c0, c1):
+        ts(T.wc[:, c0:c1], T.wr[:, c0:c1], EPS, None, A.max, None, [rg("wr", c0, c1)], [rg("wc", c0, c1)])
+
+    def copy_slots(frm, to, c0, c1):
+        for k in ("c", "s"):
+            a, b = frm + k, to + k
+            i, o = T[a][:, c0:c1], T[b][:, c0:c1]
+            if k == "c":
+                i, o = i.bitcast(dt.uint8), o.bitcast(dt.uint8)
+            dma("y", o, i, [rg(a, c0, c1)], [rg(b, c0, c1)])
+
+    def turn(t):
+        tb, sr = ("tsb" if t < 3 else "tsf"), "srow%d" % t
+        tr(tb, 0, sr, 16, 128)
+        tr(tb, 128, sr, 0, 160)
+        return tb
+
+    def in_order(out, wr, src, n, k):
+        ts(out, T[src][:, 0:n].indirect(T.co[:, k:k + 1]), 256.0, None, A.add, None, [rg(src, 0, n), rg("co", k, k + 1)], wr)
+
+    def iota(b, c0, c1, pattern, base, cm, p0=0, p1=128):
+        do("g", lambda: g.iota(T[b][p0:p1, c0:c1], pattern, base, cm, allow_small_or_imprecise_dtypes=True), [], [rg(b, c0, c1, p0, p1)])
+
+    def g_tables(u):
+        iota("cw%d" % u, 0, 272, [[0, 272]], -1000, 0)
+        iota("cw%d" % u, 16, 112, [[1, K]], NS[u] - 256, 0)
+        iota("win%d" % u, 0, 128, [[0, 128]], 0, 0)
+
+    def g_pads(u):
+        for c in (0, 144):
+            iota("srow%d" % u, c, c + 16, [[0, 16]], 0, 0)
+
+    for h in range(2):
+        dma("y", T.cb[:, 2 * P * h:2 * P * h + 2 * P], T.c[:, 2 * P * h:2 * P * h + 2 * P], [], [rg("cb", 2 * P * h, 2 * P * h + 2 * P)])
+    dma("s", T.qb[:, 0:16], T.qt[:, 0:16], [], [rg("qb", 0, 16)])
+    dma("y", T.wb[:], T.w[:], [rg("cb", 0, 4 * P)], [rg("wb", 0, 512 * O)])
+    fill("cz", 0, 96, 0.0)
+    fill("qb", 16, 512, 0.0)
+    for t in range(R):
+        fill("qoff", 8 * t, 8 * t + 8, t)
+    fill("srow0", 0, 16, 0.0)
+    fill("srow0", 144, 160, 0.0)
+    fill("win0", 0, 128, 0.0)
+    fill("cw0", 0, 272, -1000.0)
+    for a in range(4):
+        iota("s8", 0, 8, [[128 * (1 - 2 * (a // 2)), 2], [64 * (1 - 2 * (a % 2)), 2], [1, 2]], 64 * a, 2, 32 * a, 32 * a + 32)
+    iota("iot", 0, P, [[1, P]], -256, 0)
+    iota("cz", 0, 16, [[32, 4], [160, 2], [16, 2]], 0, 0)
+    iota("cz", 16, 32, [[32, 4], [-128, 2], [16, 2]], 128, 0)
+    iota("p2", 0, 1, [[0, 1]], -256, 2)
+
+    quantize("q", 0, 128, "qb")
+    for t in range(R):
+        pick_scales("qr", 128 * t, "q", 128, "qoff", 8 * t, 128)
+    pick_codes("qr", 0, "q", 128, "qoff", 0, 128)
+    cp("v", "hl", (0, 8), "s8", (0, 8))
+    do("v", lambda: g.vector.tensor_copy(T.srow0[:, 16:144], T.iot[:, 0:P].indirect(T.hl[:, 0:8])), [rg("iot", 0, P), rg("hl", 0, 8)], [rg("srow0", 16, 144)])
+    tw = turn(0)
+    tr("ctr", 0, "cz", 0, 32)
+    cp("v", "co", (0, 1), "ctr", (0, 1))
+    in_order(T.fl[:, 0:16], [rg("fl", 0, 16)], tw, 288, 0)
+    do("s", lambda: g.scalar.activation(T.pr[:, 0:P], T.iot[:, 0:P].indirect(T.fl[:, 0:16]), AF.Copy), [rg("iot", 0, P), rg("fl", 0, 16)], [rg("pr", 0, P)])
+    for h in range(2):
+        quantize("w0", 128 * h, 128, "cb")
+        mm("ps%d" % h, "qr", 0, "w0", 128 * h, 128)
+        square("wr", 128 * h, "ps%d" % h, 0, 128)
+    send_codes(0, "h", 0, "w0", P)
+    iota("cz", 32, 38, [[1, 3], [4, 2]], 0, 0)
+    iota("cz", 48, 54, [[1, 3], [-3, 2]], 3, 0)
+    iota("cz", 64, 80, [[160, 2], [32, 4], [16, 2]], 0, 0)
+    iota("cz", 80, 96, [[-128, 2], [32, 4], [16, 2]], 128, 0)
+    iota("cw0", 16, 112, [[1, K]], NS[0] - 256, 0)
+    g_pads(1)
+    pick_codes("qr", 128, "q", 128, "qoff", 8, 128)
+    ts(T.mm[:, 0:P], T.pr[:, 0:P], T.p2[:, 0:1], 1.0 - 2.0 ** -24, A.is_gt, A.max, [rg("pr", 0, P), rg("p2", 0, 1)], [rg("mm", 0, P)])
+    for h in range(2):
+        lift(128 * h, 128 * h + 128)
+
+    def y_gather(q, t, o, h):
+        n = NS[t + 1]
+        b, s, f = "yb%d" % t, "yp%d" % o, "fy%d" % t
+        out = T[b][:, P * o + h:P * o + P:2]
+        win = T[s][:, 0:n].indirect(T[f][:, 8 * h:8 * h + 8])
+        rd, wr = [rg(s, 0, n), rg(f, 8 * h, 8 * h + 8)], [rg(b, P * o, P * o + P, 0, 128, h)]
+        if q == "v":
+            do("v", lambda: g.vector.tensor_copy(out, win), rd, wr)
+        else:
+            do("s", lambda: g.scalar.activation(out, win, AF.Copy), rd, wr)
+
+    def y_store(t, o0, o1):
+        dma("y", T.y[:, P * (O * t + o0):P * (O * t + o1)], T["yb%d" % t][:, P * o0:P * o1], [rg("yb%d" % t, P * o0, P * o1)], [])
+
+    def new_products(t):
+        for o in range(O):
+            mm("ps%d" % (2 + o), "wt", 128 * o, "w%d" % (t + 1), NS[t] - 32 if t < 3 else 0, 128)
+
+    def new_copy(t, q, o):
+        cp(q, "yp%d" % o, (NS[t], NS[t + 1]), "ps%d" % (2 + o), (32, 128))
+
+    for t in range(R):
+        n = NS[t]
+        wn, tb, sr, cw, ls = "win%d" % t, ("ttb" if t < 3 else "ttf"), "srow%d" % t, "cw%d" % t, "lst%d" % t
+        do("s", lambda: g.scalar.activation(T.u64[:, 0:64], T.wc[:, 0:n].indirect(T.fl[:, 0:4]), AF.Copy), [rg("wc", 0, n), rg("fl", 0, 16)], [rg("u64", 0, 64)])
+        if t == 1:
+            for o in range(O):
+                cp("s", "yp%d" % o, (0, P), "ps%d" % (5 + o), (0, P))
+        elif t > 1:
+            for o in range(O):
+                new_copy(t - 1, "s", o)
+        tt(T.rr[:, 0:P], T.wc[:, 0:n].indirect(T.fl[:, 0:16]), T.mm[:, 0:P], A.mult, [rg("wc", 0, n), rg("fl", 0, 16), rg("mm", 0, P)], [rg("rr", 0, P)])
+        tr("t4", 0, "u64", 0, 64)
+        for e in range(2):
+            ts(T["c%d" % e][:, 0:P], T.rr[:, 0:P], T.t4[:, 32 * e:32 * e + 1], None, A.is_lt, None, [rg("rr", 0, P), rg("t4", 32 * e, 32 * e + 1)], [rg("c%d" % e, 0, P)])
+        for e in range(2):
+            do("v", lambda: g.vector.tensor_tensor_scan(T.kk[:, 128 * e:128 * e + 128], T["c%d" % e][:, 0:128], T["c%d" % e][:, 128:256], float(e - 1), A.add, A.add),
+               [rg("c%d" % e, 0, P)], [rg("kk", 128 * e, 128 * e + 128)])
+        cnt = (127, 256, 128)
+        cp("v", "r8", (2, 4), "kk", cnt, (64, 96), (96, 128))
+        cp("s", "r8", (2, 4), "kk", cnt, (0, 32), (32, 64))
+        cp("v", "r8", (2, 4), "kk", cnt, (96, 128), (64, 96))
+        cp("s", "r8", (2, 4), "kk", cnt, (32, 64), (0, 32))
+        cp("v", "r8", (0, 2), "kk", cnt)
+        if t == 0:
+            tr("ctr", 32, "cz", 32, 64)
+        for o0, o1, i0, i1, c in ((0, 64, 64, 128, 4), (64, 128, 0, 64, 4), (0, 128, 0, 128, 0)):
+            ts(T.off[o0:o1, c:c + 4], T.r8[i0:i1, 0:4], 16.0, None, A.add, None, [rg("r8", 0, 4, i0, i1)], [rg("off", c, c + 4, o0, o1)])
+        if t == 1:
+            for o in range(O):
+                new_copy(0, "s", o)
+        for o, h in (((0, 0),) if t == 1 else ((0, 0), (0, 1), (1, 0)) if t > 1 else ()):
+            y_gather("s", t - 1, o, h)
+        if t == 0:
+            cp("v", "co", (2, 6, 2), "ctr", (32, 96, 32))
+        do("v", lambda: g.vector.tensor_copy(T[wn][:, 0:272].indirect(T.off[:, 0:8]), T[sr][:, 16:144]), [rg(sr, 16, 144), rg("off", 0, 8)], [rg(wn, 0, 272)])
+        tr(tb, 0, wn, 16, 96)
+        tr(tb, 96, wn, 0, 128)
+        tt(T.a7[:, 0:7], T[tb][:, 0:224:32], T[tb][:, 16:224:32], A.add, [rg(tb, 0, 224)], [rg("a7", 0, 7)])
+        in_order(T[ls][:, 0:16], [rg(ls, 0, 16)], "a7", 7, 2)
+        nx = "w%d" % (t + 1)
+        if t == 0:
+            send(0, T.alst[:, 0:6], T.lst0[:, 0:6], [rg("lst0", 0, 6)], [rg("alst", 0, 6)], "al", "ll")
+        else:
+            pick_codes("out%d" % t, 0, "w%d" % t, n, ls, 0, K)
+            pick_scales("out%d" % t, 0, "w%d" % t, n, ls, 0, K)
+            send_codes(t, nx, n if t < 3 else 32, "out%d" % t, K)
+
+        if t == 1:
+            pick_codes("qr", 256, "q", 128, "qoff", 16, 128)
+        if t < 3:
+            mm("ps0", "qr", 128 * (t + 1), "w%d" % t, 0, n)
+            square("sq", 0, "ps0", 0, n)
+        if t == 0:
+            mm("ps1", "qr", 128, "h", 0, P)
+            square("hq", 0, "ps1", 0, P)
+        if t < 3:
+            g_tables(t + 1)
+            g_pads(t + 2)
+        sn = "srow%d" % (t + 1)
+        tt(T[sn][:, 16:144], T[cw][:, 0:272].indirect(T.off[:, 0:8]), T[sr][:, 16:144], A.max, [rg(cw, 0, 272), rg("off", 0, 8), rg(sr, 16, 144)], [rg(sn, 16, 144)])
+        tw = turn(t + 1)
+        if t < 3:
+            in_order(T.fl[:, 0:16], [rg("fl", 0, 16)], tw, 288, 0)
+        fy = "fy%d" % t
+        in_order(T[fy][:, 0:16], [rg(fy, 0, 16)], tw, 288, 4)
+        if t < 3:
+            for a in range(1, 4):
+                dma("y", T[fy][32 * a:32 * a + 32, 0:16], T[fy][0:32, 0:16], [rg(fy, 0, 16, 0, 32)], [rg(fy, 0, 16, 32 * a, 32 * a + 32)])
+            tt(T.wr[:, 0:n], T.wr[:, 0:n], T.sq[:, 0:n], A.add, [rg("wr", 0, n), rg("sq", 0, n)], [rg("wr", 0, n)])
+            lift(0, n)
+        else:
+            for a in range(1, 4):
+                cp("v", fy, (0, 16), fy, (0, 16), (32 * a, 32 * a + 32), (0, 32))
+        if t == 0:
+            for o in range(O):
+                quantize("wt", 128 * o, 128, "wb")
+                mm("ps%d" % (5 + o), "wt", 128 * o, "w0", 0, P)
+            copy_slots("w0", "w1", 0, P)
+            copy_slots("w0", "w4", 0, 32)
+        elif t == 1:
+            pick_codes("qr", 384, "q", 128, "qoff", 24, 128)
+            for o, h in ((0, 1), (1, 0), (1, 1), (2, 0), (2, 1)):
+                y_gather("s", 0, o, h)
+        else:
+            if t == 3:
+                y_store(2, 0, 1)
+            for o, h in ((1, 1), (2, 0), (2, 1)):
+                y_gather("s", t - 1, o, h)
+            if t == 3:
+                y_store(2, 1, 3)
+        if t < 3:
+            if t == 0:
+                do("s", lambda: g.scalar.activation(T.wr[:, n:n + K], T.hq[:, 0:P].indirect(T.alst[:, 0:6]), AF.Copy), [rg("hq", 0, P), rg("alst", 0, 6)], [rg("wr", n, n + K)])
+                pick_codes("w1", n, "h", P, "alst", 0, K)
+                pick_scales("w1", n, "h", P, "alst", 0, K)
+            else:
+                mm("ps1", "qr", 128 * (t + 1), nx, n - 32, 128)
+                square("wr", n, "ps1", 32, K)
+            lift(n, n + K)
+            if t == 0:
+                for u in range(2, R):
+                    copy_slots("w0", "w%d" % u, 0, P)
+            for u in range(t + 2, R):
+                copy_slots(nx, "w%d" % u, n, n + K)
+            if t > 0:
+                y_store(t - 1, 0, O)
+        new_products(t)
+    new_copy(3, "s", 0)
+    y_gather("s", 3, 0, 0)
+    y_gather("v", 3, 0, 1)
+    new_copy(3, "v", 1)
+    new_copy(3, "s", 2)
+    y_gather("v", 3, 1, 0)
+    y_gather("s", 3, 1, 1)
+    y_gather("v", 3, 2, 0)
+    y_gather("s", 3, 2, 1)
+    for o in range(O):
+        y_store(3, o, o + 1)
+
+    for sem in count:
+        if waited["g"].get(sem, 0) < count[sem]:
+            g.wait_ge(T.sem[sem], count[sem])

@@ -1,37 +1,46 @@
+from concourse.bass import DstId, RemoteDMATransfer
 from concourse.mybir import dt, AluOpType as A, ActivationFunctionType as AF
 
 P, K, R, O = 256, 96, 4, 3
 PART = [1, 2, 4, 1]
 NS = [P + K * t for t in range(R + 1)]
 EPS = 2.0 ** -125
+WIN = 1.0 - 2.0 ** -24
+AHEAD = (1, 2)
 
 SCRATCH = {"cb": ("sbuf", [128, 4 * P], "bfloat16"), "qb": ("sbuf", [128, 512], "bfloat16"), "wb": ("sbuf", [128, 512 * O], "bfloat16")}
-SEMAPHORES = ["sg", "sv", "ss", "st", "al", "ll"] + ["d%d" % i for i in range(48)]
-for _b, _n in (("q", 128), ("qr", 128 * R), ("wt", 128 * O), ("w4", 128), ("h", P), ("out1", K), ("out2", K), ("out3", K)):
+SEMAPHORES = ["sv", "ss", "st", "aq", "lq"] + ["d%d" % i for i in range(48)] + ["g%d" % i for i in range(40)]
+for _b, _n in (("q", 128), ("qr", 128 * R), ("qa", 16), ("qx", 128), ("wt", 128 * O)):
     SCRATCH[_b + "c"] = ("sbuf", [128, _n], "float8_e4m3fn_x4")
     SCRATCH[_b + "s"] = ("sbuf", [128, _n], "uint8")
 for _t in range(R):
-    SCRATCH["w%dc" % _t] = ("sbuf", [128, NS[_t]], "float8_e4m3fn_x4")
-    SCRATCH["w%ds" % _t] = ("sbuf", [128, NS[_t]], "uint8")
+    for _b, _n in (("w%d" % _t, NS[_t]), ("out%d" % _t, K if _t < 3 else 2 * K)):
+        SCRATCH[_b + "c"] = ("sbuf", [128, _n], "float8_e4m3fn_x4")
+        SCRATCH[_b + "s"] = ("sbuf", [128, _n], "uint8")
     SCRATCH["yb%d" % _t] = ("sbuf", [128, O * P], "float32")
-    SCRATCH["cw%d" % _t] = ("sbuf", [128, 272], "float32")
-    SCRATCH["fy%d" % _t] = ("sbuf", [128, 16], "uint16")
-    SCRATCH["win%d" % _t] = ("sbuf", [128, 272], "bfloat16" if _t < 3 else "float32")
+    SCRATCH["u%d" % _t] = ("sbuf", [128, NS[_t]], "float32")
+    SCRATCH["l%d" % _t] = ("sbuf", [128, NS[_t]], "float32")
+    SCRATCH["win%d" % _t] = ("sbuf", [128, 272], "bfloat16" if _t == 0 else "float32")
     SCRATCH["lst%d" % _t] = ("sbuf", [128, 16], "uint16")
-    SEMAPHORES += ["ac%d" % _t, "as%d" % _t, "lc%d" % _t, "ls%d" % _t]
-for _t in range(R + 1):
-    SCRATCH["srow%d" % _t] = ("sbuf", [128, 160], "bfloat16" if _t < 3 else "float32")
+    SCRATCH["tab%d" % (_t + 1)] = ("sbuf", [128, 48], "uint16")
+    SCRATCH["xo%d" % _t] = ("sbuf", [128, 4], "float32")
+    SCRATCH["xa%d" % _t] = ("sbuf", [128, 4], "float32")
+    SEMAPHORES += ["ac%d" % _t, "as%d" % _t, "lc%d" % _t, "ls%d" % _t, "ax%d" % _t, "lx%d" % _t]
+SCRATCH["tab0"] = ("sbuf", [128, 48], "uint16")
 for _o in range(O):
     SCRATCH["yp%d" % _o] = ("sbuf", [128, NS[4]], "float32")
 for _b in range(8):
     SCRATCH["ps%d" % _b] = ("psum", [128, 512], "float32")
-for _b, _n in (("wr", NS[3]), ("wc", NS[3]), ("sq", 512), ("hq", P), ("u64", 64), ("t4", 64), ("rr", P), ("mm", P), ("pr", P), ("p2", 8), ("iot", P),
-               ("ttf", 224), ("tsf", 288), ("a7", 8), ("s8", 8), ("cz", 96), ("ctr", 96)):
+for _b, _n in (("xs", NS[2]), ("u64", 64), ("t4", 64), ("rr", 128), ("rw", 128), ("mm", 128), ("pr", 128), ("col", 16), ("ci", 96), ("ct", 96),
+               ("cz", 160), ("ctr", 160), ("cw", 272), ("srow0", 64), ("srow1", 64), ("g1", 32), ("pay", 32), ("pf", 224), ("sa", 32), ("sb", 32),
+               ("z7", 8), ("gt", 96), ("bc", K), ("r3", 32)):
     SCRATCH[_b] = ("sbuf", [128, _n], "float32")
-for _b, _n in (("ttb", 224), ("tsb", 288), ("c0", P), ("c1", P), ("kk", P), ("r8", 8)):
+for _b, _n in (("c0", P), ("c1", P), ("kk", P), ("pb", 224)):
     SCRATCH[_b] = ("sbuf", [128, _n], "bfloat16")
-for _b, _n in (("qoff", 8 * R), ("off", 8), ("hl", 8), ("co", 8), ("fl", 16), ("alst", 8)):
+for _b, _n in (("qoff", 8 * R + 8), ("off", 2), ("co", 6), ("bl", 6)):
     SCRATCH[_b] = ("sbuf", [128, _n], "uint16")
+FL, FY, UL, PL = 0, 16, 32, 36
+C_P, C_A, C_N, C_X, C_M, C_W, C_S, C_T = range(8)
 
 
 def rank_program(g, core, T, topo):
@@ -39,24 +48,43 @@ def rank_program(g, core, T, topo):
     if rank is None:
         return
     Q = {"g": g, "v": g.vector, "s": g.scalar, "t": g.tensor, "y": g.sync}
-    own = {"g": "sg", "v": "sv", "s": "ss", "t": "st"}
+    own = {"v": "sv", "s": "ss", "t": "st"}
     count = {}
     waited = {q: {} for q in Q}
     recs = {}
-    ndma = [0]
+    used = {"d": 0, "g": 0}
 
-    def rg(b, c0, c1, p0=0, p1=128, lane=None):
-        return (b, c0, c1, p0, p1, lane)
+    def V(b, c0, c1, step=1, p0=0, p1=128):
+        return (b, c0, c1, step, p0, p1)
+
+    def ap(r):
+        if not isinstance(r, tuple):
+            return r
+        if len(r) == 2:
+            return ap(r[0]).indirect(ap(r[1]))
+        return T[r[0]][r[4]:r[5], r[1]:r[2]:r[3]] if r[3] > 1 else T[r[0]][r[4]:r[5], r[1]:r[2]]
+
+    def flat(rs):
+        out = []
+        for r in rs:
+            if isinstance(r, tuple):
+                out += list(r) if len(r) == 2 else [r]
+        return out
+
+    def cols(r):
+        return set(range(r[1], r[2], r[3]))
 
     def meets(a, b):
-        if a[0][:2] == "ps":
-            return True
-        if a[5] is not None and b[5] is not None and a[5] != b[5]:
-            return False
-        return a[1] < b[2] and b[1] < a[2] and a[3] < b[4] and b[3] < a[4]
+        return a[0][:2] == "ps" or (a[4] < b[5] and b[4] < a[5] and len(cols(a) & cols(b)) > 0)
 
     def covers(a, b):
-        return a[0][:2] == "ps" or (a[5] is None and a[1] <= b[1] and a[2] >= b[2] and a[3] <= b[3] and a[4] >= b[4])
+        return a[0][:2] == "ps" or (a[4] <= b[4] and a[5] >= b[5] and cols(b) <= cols(a))
+
+    def gate(q, sem, n=None):
+        n = n or count[sem]
+        if waited[q].get(sem, 0) < n:
+            Q[q].wait_ge(T.sem[sem], n)
+            waited[q][sem] = n
 
     def need(q, reads, writes):
         w = {}
@@ -65,15 +93,13 @@ def rank_program(g, core, T, topo):
                 for (x, xq, sem, n, xw) in recs.get(r[0], []):
                     if not (wr or xw) or not meets(r, x):
                         continue
-                    if wr and not xw and xq == q and q != "y":
+                    if wr and not xw and xq == q and q not in "yg":
                         continue
                     if r[0][:2] == "ps" and xq == q:
                         continue
                     w[sem] = max(w.get(sem, 0), n)
         for sem in w:
-            if waited[q].get(sem, 0) < w[sem]:
-                Q[q].wait_ge(T.sem[sem], w[sem])
-                waited[q][sem] = w[sem]
+            gate(q, sem, w[sem])
 
     def note(q, sem, n, reads, writes):
         for r in writes:
@@ -81,310 +107,378 @@ def rank_program(g, core, T, topo):
         for r in writes:
             recs.setdefault(r[0], []).append((r, q, sem, n, True))
         for r in reads:
-            recs.setdefault(r[0], []).append((r, q, sem, n, False))
+            recs.setdefault(r[0], []).append((r, q, sem, n, r[0][:2] == "ps"))
+
+    def fresh(kind):
+        used[kind] += 1
+        return "%s%d" % (kind, used[kind] - 1)
 
     def do(q, call, reads, writes):
+        reads = flat(reads)
         need(q, reads, writes)
-        if q == "g" and count.get("sg", 0) > waited["g"].get("sg", 0):
-            g.wait_ge(T.sem.sg, count["sg"])
-            waited["g"]["sg"] = count["sg"]
-        ins = call()
-        sem = own[q]
+        sem = own[q] if q in own else fresh("g")
         count[sem] = count.get(sem, 0) + 1
-        ins.then_inc(T.sem[sem], 1)
+        call().then_inc(T.sem[sem], 1)
         note(q, sem, count[sem], reads, writes)
 
-    def dma(q, out, in_, reads, writes):
+    def raw(r):
+        return ap(r).bitcast(dt.uint8) if SCRATCH[r[0]][2] == "float8_e4m3fn_x4" else ap(r)
+
+    def dma(q, out, in_, reads, writes, add=False):
         need(q, reads, writes)
-        sem = "d%d" % ndma[0]
-        ndma[0] += 1
-        Q[q].dma_start(out, in_).then_inc(T.sem[sem], 16)
+        sem = fresh("d")
+        ins = g.dma_start(out, in_, accum_op=A.add) if add else Q[q].dma_start(out, in_)
+        ins.then_inc(T.sem[sem], 16)
         count[sem] = 16
         note("y" if q == "y" else q + "d", sem, 16, reads, writes)
 
-    def send(t, out, in_, reads, writes, sa, sl):
+    def send(t, o, i, sa, sl):
         dst = T.cores[rank ^ PART[t]]
         rid, pid, _ = topo.addr(dst)
-        need("g", reads, [])
-        g.remote_dma(out, in_, T.sem[sa], T.sem[sl], pid, rid, topo.mask(core, dst))
+        need("g", [i], [])
+        g.remote_dma(raw(o), raw(i), T.sem[sa], T.sem[sl], pid, rid, topo.mask(core, dst))
         count[sl] = len(topo.engines(core, dst))
         count[sa] = len(topo.engines(dst, core))
-        note("r", sa, count[sa], [], writes)
+        note("r", sa, count[sa], [], [o])
 
-    def send_codes(t, ob, o0, ib, n):
-        for k in ("c", "s"):
-            i, o = T[ib + k][:, 0:n], T[ob + k][:, o0:o0 + n]
-            if k == "c":
-                i, o = i.bitcast(dt.uint8), o.bitcast(dt.uint8)
-            send(t, o, i, [rg(ib + k, 0, n)], [rg(ob + k, o0, o0 + n)], "a%s%d" % (k, t), "l%s%d" % (k, t))
+    def landing(t):
+        return ("w%d" % (t + 1), NS[t]) if t < 3 else ("out3", K)
 
-    def cp(q, ob, oc, ib, ic, p=(0, 128), ip=None):
-        ip = ip or p
-        o = T[ob][p[0]:p[1], slice(*oc)]
-        i = T[ib][ip[0]:ip[1], slice(*ic)]
-        rd = [rg(ib, ic[0], ic[1], ip[0], ip[1])]
-        wr = [rg(ob, oc[0], oc[1], p[0], p[1], (oc[0] % oc[2]) if len(oc) > 2 else None)]
+    def send_codes(t):
+        nx, n = landing(t)
+        for k in "cs":
+            send(t, V(nx + k, n, n + K), V("out%d%s" % (t, k), 0, K), "a%s%d" % (k, t), "l%s%d" % (k, t))
+
+    def left(q, t):
+        gate(q, "lc%d" % t)
+        gate(q, "ls%d" % t)
+
+    def cp(q, o, i):
         if q == "v":
-            do("v", lambda: g.vector.tensor_copy(o, i), rd, wr)
+            wr = [o[0]] if len(o) == 2 else [o]
+            do("v", lambda: g.vector.tensor_copy(ap(o), ap(i)), [i] + ([o[1]] if len(o) == 2 else []), wr)
         else:
-            do("s", lambda: g.scalar.activation(o, i, AF.Copy), rd, wr)
+            do("s", lambda: g.scalar.activation(ap(o), ap(i), AF.Copy), [i], [o])
 
-    def ts(out, in0, s1, s2, op0, op1, rd, wr):
+    def ts(o, i, s1, op0, s2=None, op1=None):
         if op1 is None:
-            do("v", lambda: g.vector.tensor_scalar(out, in0, s1, None, op0), rd, wr)
+            do("v", lambda: g.vector.tensor_scalar(ap(o), ap(i), ap(s1), None, op0), [i, s1], [o])
         else:
-            do("v", lambda: g.vector.tensor_scalar(out, in0, s1, s2, op0, op1), rd, wr)
+            do("v", lambda: g.vector.tensor_scalar(ap(o), ap(i), ap(s1), ap(s2), op0, op1), [i, s1, s2], [o])
 
-    def tt(out, a, b, op, rd, wr):
-        do("v", lambda: g.vector.tensor_tensor(out, a, b, op), rd, wr)
+    def tt(o, a, b, op):
+        do("v", lambda: g.vector.tensor_tensor(ap(o), ap(a), ap(b), op), [a, b], [o])
 
-    def fill(b, c0, c1, v):
-        do("v", lambda: g.vector.memset(T[b][:, c0:c1], v), [], [rg(b, c0, c1)])
+    def fill(o, v):
+        do("v", lambda: g.vector.memset(ap(o), v), [], [o])
 
-    def tr(ob, o0, ib, i0, n):
-        do("v", lambda: g.vector.transpose(T[ob][:, o0:o0 + n], T[ib][:, i0:i0 + n]), [rg(ib, i0, i0 + n)], [rg(ob, o0, o0 + n)])
+    def tr(o, i):
+        do("v", lambda: g.vector.transpose(ap(o), ap(i)), [i], [o])
 
-    def pick_codes(ob, o0, ib, n, lb, l0, k):
-        c, oc = ib + "c", ob + "c"
-        do("v", lambda: g.vector.tensor_copy(T[oc][:, o0:o0 + k].bitcast(dt.uint32), T[c][:, 0:n].bitcast(dt.uint32).indirect(T[lb][:, l0:l0 + k // 16])),
-           [rg(c, 0, n), rg(lb, l0, l0 + k // 16)], [rg(oc, o0, o0 + k)])
+    def iota(o, pattern, base=0, cm=0):
+        if o[5] - o[4] < 128 or used.get("part"):
+            for i in range(used["g"]):
+                gate("g", "g%d" % i)
+        used["part"] = o[5] - o[4] < 128
+        do("g", lambda: g.iota(ap(o), pattern, base, cm, allow_small_or_imprecise_dtypes=True), [], [o])
 
-    def pick_scales(ob, o0, ib, n, lb, l0, k):
-        s, os_ = ib + "s", ob + "s"
-        do("s", lambda: g.scalar.activation(T[os_][:, o0:o0 + k], T[s][:, 0:n].indirect(T[lb][:, l0:l0 + k // 16]), AF.Copy),
-           [rg(s, 0, n), rg(lb, l0, l0 + k // 16)], [rg(os_, o0, o0 + k)])
+    def pick_codes(ob, o0, ib, n, lst):
+        o, i = V(ob + "c", o0, o0 + 16 * (lst[2] - lst[1])), V(ib + "c", 0, n)
+        do("v", lambda: g.vector.tensor_copy(ap(o).bitcast(dt.uint32), ap(i).bitcast(dt.uint32).indirect(ap(lst))), [i, lst], [o])
+
+    def pick_scales(ob, o0, ib, n, lst):
+        cp("s", V(ob + "s", o0, o0 + 16 * (lst[2] - lst[1])), (V(ib + "s", 0, n), lst))
 
     def mm(bank, lc, l0, rc, r0, n):
-        lh, ls, rh, rs = T[lc + "c"], T[lc + "s"], T[rc + "c"], T[rc + "s"]
-        do("t", lambda: g.tensor.matmul_mx(T[bank][:, 0:n], lh[:, l0:l0 + 128], ls[:, l0:l0 + 128], rh[:, r0:r0 + n], rs[:, r0:r0 + n], True, True),
-           [rg(lc + "c", l0, l0 + 128), rg(lc + "s", l0, l0 + 128), rg(rc + "c", r0, r0 + n), rg(rc + "s", r0, r0 + n)], [rg(bank, 0, 512)])
+        ins = [V(lc + "c", l0, l0 + 128), V(lc + "s", l0, l0 + 128), V(rc + "c", r0, r0 + n), V(rc + "s", r0, r0 + n)]
+        b = "ps%d" % bank
+        do("t", lambda: g.tensor.matmul_mx(T[b][:, 0:n], ap(ins[0]), ap(ins[1]), ap(ins[2]), ap(ins[3]), True, True), ins, [V(b, 0, 512)])
 
-    def quantize(ob, o0, n, ib):
-        c, s = T[ob + "c"], T[ob + "s"]
-        do("v", lambda: g.vector.quantize_mx(c[:, o0:o0 + n], s[:, o0:o0 + n], T[ib][:, 4 * o0:4 * (o0 + n)]),
-           [rg(ib, 4 * o0, 4 * (o0 + n))], [rg(ob + "c", o0, o0 + n), rg(ob + "s", o0, o0 + n)])
+    def mm_new(bank, lc, l0, t):
+        nx, n = landing(t)
+        mm(bank, lc, l0, nx, n - 32, 128)
 
-    def square(ob, o0, bank, i0, n):
-        do("s", lambda: g.scalar.activation(T[ob][:, o0:o0 + n], T[bank][:, i0:i0 + n], AF.Square), [rg(bank, 0, 512)], [rg(ob, o0, o0 + n)])
+    def quantize(ob, o0, ib):
+        c, s, i = V(ob + "c", o0, o0 + 128), V(ob + "s", o0, o0 + 128), V(ib, 4 * o0, 4 * o0 + 512)
+        do("v", lambda: g.vector.quantize_mx(ap(c), ap(s), ap(i)), [i], [c, s])
 
-    def lift(c0, c1):
-        ts(T.wc[:, c0:c1], T.wr[:, c0:c1], EPS, None, A.max, None, [rg("wr", c0, c1)], [rg("wc", c0, c1)])
+    def square(ob, c0, c1, bank, i0):
+        o, i = V(ob, c0, c1), V("ps%d" % bank, i0, i0 + c1 - c0)
+        do("s", lambda: g.scalar.activation(ap(o), ap(i), AF.Square), [i], [o])
+
+    def lift(t, c0, c1):
+        ts(V("l%d" % t, c0, c1), V("u%d" % t, c0, c1), EPS, A.max)
+
+    def add(t, c0, c1):
+        tt(V("u%d" % t, c0, c1), V("u%d" % t, c0, c1), V("u%d" % (t - 1), c0, c1), A.add)
+
+    def add_dma(t, c0, c1):
+        o, i = V("u%d" % t, c0, c1), V("u%d" % (t - 1), c0, c1)
+        dma("g", ap(o), ap(i), [i, o], [o], add=True)
 
     def copy_slots(frm, to, c0, c1):
-        for k in ("c", "s"):
-            a, b = frm + k, to + k
-            i, o = T[a][:, c0:c1], T[b][:, c0:c1]
-            if k == "c":
-                i, o = i.bitcast(dt.uint8), o.bitcast(dt.uint8)
-            dma("y", o, i, [rg(a, c0, c1)], [rg(b, c0, c1)])
+        for k in "cs":
+            i, o = V(frm + k, c0, c1), V(to + k, c0, c1)
+            dma("y", raw(o), raw(i), [i], [o])
 
-    def turn(t):
-        tb, sr = ("tsb" if t < 3 else "tsf"), "srow%d" % t
-        tr(tb, 0, sr, 16, 128)
-        tr(tb, 128, sr, 0, 160)
-        return tb
+    def col(k):
+        return V("col", k, k + 1)
 
-    def in_order(out, wr, src, n, k):
-        ts(out, T[src][:, 0:n].indirect(T.co[:, k:k + 1]), 256.0, None, A.add, None, [rg(src, 0, n), rg("co", k, k + 1)], wr)
-
-    def iota(b, c0, c1, pattern, base, cm, p0=0, p1=128):
-        do("g", lambda: g.iota(T[b][p0:p1, c0:c1], pattern, base, cm, allow_small_or_imprecise_dtypes=True), [], [rg(b, c0, c1, p0, p1)])
-
-    def g_tables(u):
-        iota("cw%d" % u, 0, 272, [[0, 272]], -1000, 0)
-        iota("cw%d" % u, 16, 112, [[1, K]], NS[u] - 256, 0)
-        iota("win%d" % u, 0, 128, [[0, 128]], 0, 0)
-
-    def g_pads(u):
-        for c in (0, 144):
-            iota("srow%d" % u, c, c + 16, [[0, 16]], 0, 0)
-
-    for h in range(2):
-        dma("y", T.cb[:, 2 * P * h:2 * P * h + 2 * P], T.c[:, 2 * P * h:2 * P * h + 2 * P], [], [rg("cb", 2 * P * h, 2 * P * h + 2 * P)])
-    dma("s", T.qb[:, 0:16], T.qt[:, 0:16], [], [rg("qb", 0, 16)])
-    dma("y", T.wb[:], T.w[:], [rg("cb", 0, 4 * P)], [rg("wb", 0, 512 * O)])
-    fill("cz", 0, 96, 0.0)
-    fill("qb", 16, 512, 0.0)
-    for t in range(R):
-        fill("qoff", 8 * t, 8 * t + 8, t)
-    fill("srow0", 0, 16, 0.0)
-    fill("srow0", 144, 160, 0.0)
-    fill("win0", 0, 128, 0.0)
-    fill("cw0", 0, 272, -1000.0)
-    for a in range(4):
-        iota("s8", 0, 8, [[128 * (1 - 2 * (a // 2)), 2], [64 * (1 - 2 * (a % 2)), 2], [1, 2]], 64 * a, 2, 32 * a, 32 * a + 32)
-    iota("iot", 0, P, [[1, P]], -256, 0)
-    iota("cz", 0, 16, [[32, 4], [160, 2], [16, 2]], 0, 0)
-    iota("cz", 16, 32, [[32, 4], [-128, 2], [16, 2]], 128, 0)
-    iota("p2", 0, 1, [[0, 1]], -256, 2)
-
-    quantize("q", 0, 128, "qb")
-    for t in range(R):
-        pick_scales("qr", 128 * t, "q", 128, "qoff", 8 * t, 128)
-    pick_codes("qr", 0, "q", 128, "qoff", 0, 128)
-    cp("v", "hl", (0, 8), "s8", (0, 8))
-    do("v", lambda: g.vector.tensor_copy(T.srow0[:, 16:144], T.iot[:, 0:P].indirect(T.hl[:, 0:8])), [rg("iot", 0, P), rg("hl", 0, 8)], [rg("srow0", 16, 144)])
-    tw = turn(0)
-    tr("ctr", 0, "cz", 0, 32)
-    cp("v", "co", (0, 1), "ctr", (0, 1))
-    in_order(T.fl[:, 0:16], [rg("fl", 0, 16)], tw, 288, 0)
-    do("s", lambda: g.scalar.activation(T.pr[:, 0:P], T.iot[:, 0:P].indirect(T.fl[:, 0:16]), AF.Copy), [rg("iot", 0, P), rg("fl", 0, 16)], [rg("pr", 0, P)])
-    for h in range(2):
-        quantize("w0", 128 * h, 128, "cb")
-        mm("ps%d" % h, "qr", 0, "w0", 128 * h, 128)
-        square("wr", 128 * h, "ps%d" % h, 0, 128)
-    send_codes(0, "h", 0, "w0", P)
-    iota("cz", 32, 38, [[1, 3], [4, 2]], 0, 0)
-    iota("cz", 48, 54, [[1, 3], [-3, 2]], 3, 0)
-    iota("cz", 64, 80, [[160, 2], [32, 4], [16, 2]], 0, 0)
-    iota("cz", 80, 96, [[-128, 2], [32, 4], [16, 2]], 128, 0)
-    iota("cw0", 16, 112, [[1, K]], NS[0] - 256, 0)
-    g_pads(1)
-    pick_codes("qr", 128, "q", 128, "qoff", 8, 128)
-    ts(T.mm[:, 0:P], T.pr[:, 0:P], T.p2[:, 0:1], 1.0 - 2.0 ** -24, A.is_gt, A.max, [rg("pr", 0, P), rg("p2", 0, 1)], [rg("mm", 0, P)])
-    for h in range(2):
-        lift(128 * h, 128 * h + 128)
-
-    def y_gather(q, t, o, h):
-        n = NS[t + 1]
-        b, s, f = "yb%d" % t, "yp%d" % o, "fy%d" % t
-        out = T[b][:, P * o + h:P * o + P:2]
-        win = T[s][:, 0:n].indirect(T[f][:, 8 * h:8 * h + 8])
-        rd, wr = [rg(s, 0, n), rg(f, 8 * h, 8 * h + 8)], [rg(b, P * o, P * o + P, 0, 128, h)]
-        if q == "v":
-            do("v", lambda: g.vector.tensor_copy(out, win), rd, wr)
-        else:
-            do("s", lambda: g.scalar.activation(out, win, AF.Copy), rd, wr)
-
-    def y_store(t, o0, o1):
-        dma("y", T.y[:, P * (O * t + o0):P * (O * t + o1)], T["yb%d" % t][:, P * o0:P * o1], [rg("yb%d" % t, P * o0, P * o1)], [])
+    def qlist(t):
+        return V("qoff", 8 * t, 8 * t + 8)
 
     def new_products(t):
         for o in range(O):
-            mm("ps%d" % (2 + o), "wt", 128 * o, "w%d" % (t + 1), NS[t] - 32 if t < 3 else 0, 128)
+            mm_new(2 + o, "wt", 128 * o, t)
 
     def new_copy(t, q, o):
-        cp(q, "yp%d" % o, (NS[t], NS[t + 1]), "ps%d" % (2 + o), (32, 128))
+        cp(q, V("yp%d" % o, NS[t], NS[t + 1]), V("ps%d" % (2 + o), 32, 128))
+
+    def y_gather(q, t, *js):
+        for o, e in [divmod(j, 2) for j in js]:
+            cp(q, V("yb%d" % t, P * o + e, P * o + P, 2), (V("yp%d" % o, 0, NS[t + 1]), V("tab%d" % (t + 1), FY + 8 * e, FY + 8 * e + 8)))
+
+    def y_store(t, o0, o1):
+        i = V("yb%d" % t, P * o0, P * o1)
+        dma("y", T.y[:, P * (O * t + o0):P * (O * t + o1)], ap(i), [i], [])
+
+    H128, Q2, I1 = V("ct", 0, 1), V("ct", 32, 33), V("ct", 64, 65)
+    dma("s", T.qb[:, 0:16], T.qt[:, 0:16], [], [V("qb", 0, 16)])
+    for h in range(2):
+        dma("y", T.cb[:, 512 * h:512 * h + 512], T.c[:, 512 * h:512 * h + 512], [], [V("cb", 512 * h, 512 * h + 512)])
+    dma("y", T.wb[:], T.w[:], [V("cb", 0, 4 * P)], [V("wb", 0, 512 * O)])
+    iota(V("ci", 0, 32), [[128, 2], [0, 16]])
+    iota(V("ci", 32, 64), [[0, 2], [2, 16]])
+    iota(V("ci", 64, 96), [[1, 32]])
+    iota(col(C_P), [[0, 1]], 0, 1)
+    iota(V("pr", 0, 128), [[1, 2], [32, 4], [2, 16]])
+    fill(V("qb", 16, 512), 0.0)
+    for t in range(R):
+        fill(qlist(t), t)
+    fill(V("cz", 0, 128), 0.0)
+    fill(V("cw", 0, 272), -2000.0)
+    tr(V("ct", 0, 96), V("ci", 0, 96))
+    fill(V("win0", 0, 128), 0.0)
+    ts(col(C_A), col(C_P), I1, A.subtract)
+    ts(col(C_N), H128, -1.0, A.mult, 128.0, A.add)
+    ts(col(C_M), Q2, 16.0, A.is_lt)
+    ts(col(C_X), Q2, col(C_A), A.add)
+    ts(col(C_W), col(C_N), 1.0 / 128, A.mult, WIN, A.max)
+    for s in range(2):
+        fill(V("srow%d" % s, 0, 64), 0.0)
+    iota(V("r3", 0, 32), [[1, 2], [2, 16]])
+    iota(V("cz", 96, 102), [[1, 3], [4, 2]])
+    iota(V("cz", 112, 118), [[1, 3], [-3, 2]], 3)
+    iota(V("cw", 16, 16 + K), [[1, K]])
+
+    quantize("q", 0, "qb")
+    ts(V("tab0", FL, FL + 8), V("pr", 0, 128, 16), Q2, A.add, H128, A.add)
+    for t in range(2):
+        pick_codes("qr", 128 * t, "q", 128, qlist(t))
+    for t in range(3):
+        pick_scales("qr", 128 * t, "q", 128, qlist(t))
+    need("g", [V("qc", 0, 128), V("qs", 0, 128)], [])
+    for k in "cs":
+        trs = []
+        for j, t in enumerate(AHEAD):
+            dst = T.cores[rank ^ PART[t]]
+            rid, pid, _ = topo.addr(dst)
+            es = topo.engines(core, dst)
+            es = es[j * len(es) // 2:(j + 1) * len(es) // 2]
+            trs.append(RemoteDMATransfer(dst_ids=[DstId(rid=rid, pnc=pid)], dma_engine_mask=sum(1 << e for e in es), remote_sem=T.sem.aq,
+                                         src=raw(V("q" + k, t + 1, t + 3)), dst=raw(V("qa" + k, 2 * j, 2 * j + 2))))
+            count["lq"] = count.get("lq", 0) + len(es)
+            count["aq"] = count.get("aq", 0) + len(topo.engines(dst, core)) // 2
+        g.remote_dma_fused(trs, local_sem=T.sem.lq)
+    note("r", "aq", count["aq"], [], [V("qac", 0, 4), V("qas", 0, 4)])
+    iota(V("cz", 0, 16), [[16, 2], [64, 2], [0, 4]])
+    iota(V("cz", 16, 32), [[-16, 2], [-32, 2], [0, 4]], 48)
+    iota(V("cz", 32, 48), [[64, 2], [16, 2], [0, 4]])
+    iota(V("cz", 48, 64), [[-32, 2], [16, 2], [0, 4]], 32)
+    iota(V("cz", 64, 68), [[64, 2], [16, 2]])
+    iota(V("cz", 68, 70), [[64, 2]])
+    iota(V("cz", 84, 86), [[-32, 2]], 48)
+    for a in range(4):
+        iota(V("cz", 128, 160, 1, 32 * a, 32 * a + 32), [[0, 8], [8 - 16 * (a // 2), 2], [4 - 8 * (a % 2), 2]], 4 * a)
+    iota(V("win1", 0, 128), [[0, 128]])
+
+    quantize("w0", 0, "cb")
+    mm(0, "qr", 0, "w0", 0, 128)
+    square("u0", 0, 128, 0, 0)
+    pick_scales("qr", 384, "q", 128, qlist(3))
+    ts(V("tab0", FL + 8, FL + 16), V("pr", 0, 128, 16), Q2, A.add, col(C_N), A.add)
+    for h in range(2):
+        ts(V("tab0", UL + h, UL + 4, 2), V("pr", 0, 128, 64), col(C_X), A.add, 128.0 * h, A.add)
+    ts(V("mm", 0, 128), V("pr", 0, 128), col(C_X), A.is_gt, WIN, A.max)
+    quantize("w0", 128, "cb")
+    mm(1, "qr", 0, "w0", 128, 128)
+    square("u0", 128, 256, 1, 0)
+    pick_codes("qr", 256, "q", 128, qlist(2))
+    mm(6, "qr", 128, "w0", 0, P)
+    mm(7, "qr", 256, "w0", 0, P)
+    lift(0, 0, 128)
+    ts(col(C_S), Q2, 16.0, A.is_ge, -3.0, A.mult)
+    lift(0, 128, 256)
 
     for t in range(R):
-        n = NS[t]
-        wn, tb, sr, cw, ls = "win%d" % t, ("ttb" if t < 3 else "ttf"), "srow%d" % t, "cw%d" % t, "lst%d" % t
-        do("s", lambda: g.scalar.activation(T.u64[:, 0:64], T.wc[:, 0:n].indirect(T.fl[:, 0:4]), AF.Copy), [rg("wc", 0, n), rg("fl", 0, 16)], [rg("u64", 0, 64)])
+        n, tab, nt = NS[t], "tab%d" % t, "tab%d" % (t + 1)
+        lw, wn, ls = V("l%d" % t, 0, n), "win%d" % t, "lst%d" % t
+        sr, sn = "srow%d" % (t % 2), "srow%d" % ((t + 1) % 2)
+        pp = "pb" if t == 0 else "pf"
+        off = V("off", 0, 2)
+        ahead = t in AHEAD
+        cp("s", V("u64", 0, 64), (lw, V(tab, UL, UL + 4)))
+        cp("s", V("rw", 0, 128), (lw, V(tab, FL + 8, FL + 16)))
+        tt(V("rr", 0, 128), (lw, V(tab, FL, FL + 8)), V("mm", 0, 128), A.mult)
+        tr(V("t4", 0, 64), V("u64", 0, 64))
+        if t == 0:
+            square("u1", 0, P, 6, 0)
+            square("u2", 0, P, 7, 0)
+            ts(V("g1", 0, 32), V("r3", 0, 32), H128, A.add, col(C_A), A.add)
+        if t == 1:
+            quantize("wt", 256, "wb")
+        if ahead:
+            mm_new(0, "qx", 0, t - 1)
+            mm_new(1, "qr", 256, t - 1)
+            square("xs", NS[t - 1], n, 0, 32)
+            for o in range(O if t == 1 else 0):
+                mm(5 + o, "wt", 128 * o, "w0", 0, P)
+            mm_new(0, "qr", 384, t - 1)
+            new_products(t - 1)
+            square("u2", NS[t - 1], n, 1, 32)
+            square("u3", NS[t - 1], n, 0, 32)
         if t == 1:
             for o in range(O):
-                cp("s", "yp%d" % o, (0, P), "ps%d" % (5 + o), (0, P))
-        elif t > 1:
+                cp("s", V("yp%d" % o, 0, P), V("ps%d" % (5 + o), 0, P))
+        if t == 2:
+            lift(3, 0, 80)
+        if t == 3:
+            new_products(2)
+        if t > 0:
             for o in range(O):
                 new_copy(t - 1, "s", o)
-        tt(T.rr[:, 0:P], T.wc[:, 0:n].indirect(T.fl[:, 0:16]), T.mm[:, 0:P], A.mult, [rg("wc", 0, n), rg("fl", 0, 16), rg("mm", 0, P)], [rg("rr", 0, P)])
-        tr("t4", 0, "u64", 0, 64)
+            y_gather("s", t - 1, *range(3 if t == 1 else 4))
         for e in range(2):
-            ts(T["c%d" % e][:, 0:P], T.rr[:, 0:P], T.t4[:, 32 * e:32 * e + 1], None, A.is_lt, None, [rg("rr", 0, P), rg("t4", 32 * e, 32 * e + 1)], [rg("c%d" % e, 0, P)])
+            ts(V("c%d" % e, 0, 128), V("rr", 0, 128), V("t4", 32 * e, 32 * e + 1), A.is_lt)
         for e in range(2):
-            do("v", lambda: g.vector.tensor_tensor_scan(T.kk[:, 128 * e:128 * e + 128], T["c%d" % e][:, 0:128], T["c%d" % e][:, 128:256], float(e - 1), A.add, A.add),
-               [rg("c%d" % e, 0, P)], [rg("kk", 128 * e, 128 * e + 128)])
-        cnt = (127, 256, 128)
-        cp("v", "r8", (2, 4), "kk", cnt, (64, 96), (96, 128))
-        cp("s", "r8", (2, 4), "kk", cnt, (0, 32), (32, 64))
-        cp("v", "r8", (2, 4), "kk", cnt, (96, 128), (64, 96))
-        cp("s", "r8", (2, 4), "kk", cnt, (32, 64), (0, 32))
-        cp("v", "r8", (0, 2), "kk", cnt)
+            ts(V("c%d" % e, 128, 256), V("rw", 0, 128), col(C_W), A.mult, V("t4", 32 * e, 32 * e + 1), A.is_lt)
+        for e in range(2):
+            a, b, o = V("c%d" % e, 0, 128), V("c%d" % e, 128, 256), V("kk", 128 * e, 128 * e + 128)
+            do("v", lambda: g.vector.tensor_tensor_scan(ap(o), ap(a), ap(b), float(e - 1), A.add, A.add), [a, b], [o])
         if t == 0:
-            tr("ctr", 32, "cz", 32, 64)
-        for o0, o1, i0, i1, c in ((0, 64, 64, 128, 4), (64, 128, 0, 64, 4), (0, 128, 0, 128, 0)):
-            ts(T.off[o0:o1, c:c + 4], T.r8[i0:i1, 0:4], 16.0, None, A.add, None, [rg("r8", 0, 4, i0, i1)], [rg("off", c, c + 4, o0, o1)])
+            ts(V(sr, 16, 48), V("g1", 0, 32), col(C_M), A.mult, EPS, A.max)
         if t == 1:
-            for o in range(O):
-                new_copy(0, "s", o)
-        for o, h in (((0, 0),) if t == 1 else ((0, 0), (0, 1), (1, 0)) if t > 1 else ()):
-            y_gather("s", t - 1, o, h)
+            tt(V("pay", 0, 32), (V("xs", 0, n), V(tab, PL, PL + 2)), V(sr, 16, 48), A.max)
+        if t == 2:
+            lift(3, 80, 160)
+        ts(off, V("kk", 127, 256, 128), 16.0, A.add)
         if t == 0:
-            cp("v", "co", (2, 6, 2), "ctr", (32, 96, 32))
-        do("v", lambda: g.vector.tensor_copy(T[wn][:, 0:272].indirect(T.off[:, 0:8]), T[sr][:, 16:144]), [rg(sr, 16, 144), rg("off", 0, 8)], [rg(wn, 0, 272)])
-        tr(tb, 0, wn, 16, 96)
-        tr(tb, 96, wn, 0, 128)
-        tt(T.a7[:, 0:7], T[tb][:, 0:224:32], T[tb][:, 16:224:32], A.add, [rg(tb, 0, 224)], [rg("a7", 0, 7)])
-        in_order(T[ls][:, 0:16], [rg(ls, 0, 16)], "a7", 7, 2)
-        nx = "w%d" % (t + 1)
+            tr(V("ctr", 96, 128), V("cz", 96, 128))
+        if t == 1:
+            fill(V("bl", 2, 4), 1)
+        if t == 2:
+            tt(V("pay", 0, 32), (V("xs", 0, n), V(tab, PL, PL + 2)), V(sr, 16, 48), A.max)
+        cp("v", (V(wn, 0, 272), off), V("pay", 0, 32) if ahead else V(sr, 16, 48))
+        ts(V("g1", 0, 32), (V("cw", 0, 272), off), float(n), A.add, col(C_M), A.mult)
+        tr(V(pp, 0, 96), V(wn, 16, 112))
+        tr(V(pp, 96, 224), V(wn, 0, 128))
+        tt(V(sn, 16, 48), V("g1", 0, 32), V(sr, 16, 48), A.max)
+        r0, st = (4 * (t - 1), 8) if ahead else (0, 16)
+        m = 224 // st
+        tt(V("sa", 0, m, 1, 0, 64), V(pp, r0, 224, st, 0, 64), V(pp, r0, 224, st, 64, 128), A.add)
+        tr(V("gt", 0, 32), V(sn, 16, 48))
+        for p in (0, 32):
+            tt(V("sb", 0, m, 1, p, p + 32), V("sa", 0, m, 1, 0, 32), V("sa", 0, m, 1, 32, 64), A.add)
+        tr(V("gt", 32, 96), V(sn, 0, 64))
+        if ahead:
+            for p in (0, 64):
+                tt(V("xo%d" % t, 0, 3, 1, p, p + 64), V("sb", 1, 12, 4, 0, 64), V("sb", 3, 12, 4, 0, 64), A.add)
+            send(t, V("xa%d" % t, 0, 3), V("xo%d" % t, 0, 3), "ax%d" % t, "lx%d" % t)
+        s2 = 4 if ahead else 2
+        for p in (0, 64):
+            tt(V("z7", 0, 7, 1, p, p + 64), V("sb", 0, m, s2, 0, 64), V("sb", s2 // 2, m, s2, 0, 64), A.add)
         if t == 0:
-            send(0, T.alst[:, 0:6], T.lst0[:, 0:6], [rg("lst0", 0, 6)], [rg("alst", 0, 6)], "al", "ll")
+            cp("v", V("co", 4, 5), V("ctr", 96, 97))
         else:
-            pick_codes("out%d" % t, 0, "w%d" % t, n, ls, 0, K)
-            pick_scales("out%d" % t, 0, "w%d" % t, n, ls, 0, K)
-            send_codes(t, nx, n if t < 3 else 32, "out%d" % t, K)
+            cp("v", V("gt", 8, 96, 16, 0, 64), V("gt", 0, 96, 16, 64, 128))
+        cp("v", V(ls, 0, 16), (V("z7", 0, 7), V("co", 4, 5)))
+        if t == 0:
+            cp("v", V("gt", 8, 96, 16, 0, 64), V("gt", 0, 96, 16, 64, 128))
+        cp("s", V("gt", 8, 96, 16, 64, 128), V("gt", 0, 96, 16, 0, 64))
+        if t > 0:
+            cp("v", V("gt", 4, 96, 8, 0, 32), V("gt", 0, 96, 8, 32, 64))
+        pick_codes("out%d" % t, 0, "w%d" % t, n, V(ls, 0, 6))
+        pick_scales("out%d" % t, 0, "w%d" % t, n, V(ls, 0, 6))
+        send_codes(t)
 
+        if t == 0:
+            cp("v", V("gt", 4, 96, 8, 0, 32), V("gt", 0, 96, 8, 32, 64))
+        cp("v", V("gt", 4, 96, 8, 32, 64), V("gt", 0, 96, 8, 0, 32))
+        cp("s", V("gt", 4, 96, 8, 64, 96), V("gt", 0, 96, 8, 96, 128))
+        cp("s", V("gt", 4, 96, 8, 96, 128), V("gt", 0, 96, 8, 64, 96))
+        if t == 0:
+            ts(col(C_T), Q2, 24.0, A.is_ge, 2.0, A.mult)
+            quantize("w1", 128, "cb")
+            add(1, 0, P)
+            add_dma(2, 0, P)
+            ts(qlist(4), qlist(3), col(C_S), A.add, col(C_T), A.add)
+            pick_codes("qr", 384, "q", 128, qlist(3))
+            mm(0, "qr", 384, "w0", 0, P)
+            pick_scales("qx", 0, "qa", 4, qlist(4))
+            pick_codes("qx", 0, "qa", 4, qlist(4))
+            mm(2, "qx", 0, "w0", 0, P)
+            square("u3", 0, P, 0, 0)
+            square("xs", 0, P, 2, 0)
+            tr(V("ctr", 0, 96), V("cz", 0, 96))
+            tr(V("ctr", 128, 160), V("cz", 128, 160))
+            lift(1, 0, P)
+            ts(V("co", 0, 2), V("ctr", 0, 64, 32), V("ctr", 128, 129), A.add)
+            cp("v", V("co", 2, 3), V("ctr", 64, 65))
+            quantize("w1", 0, "cb")
         if t == 1:
-            pick_codes("qr", 256, "q", 128, "qoff", 16, 128)
-        if t < 3:
-            mm("ps0", "qr", 128 * (t + 1), "w%d" % t, 0, n)
-            square("sq", 0, "ps0", 0, n)
+            add(2, NS[0], NS[1])
+            fill(V("bl", 0, 2), 0)
+            fill(V("bl", 4, 6), 2)
+        if t == 2:
+            add(3, NS[1], NS[2])
+        cp("v", V(nt, 0, 48), (V("gt", 0, 96), V("co", 0, 3)))
         if t == 0:
-            mm("ps1", "qr", 128, "h", 0, P)
-            square("hq", 0, "ps1", 0, P)
-        if t < 3:
-            g_tables(t + 1)
-            g_pads(t + 2)
-        sn = "srow%d" % (t + 1)
-        tt(T[sn][:, 16:144], T[cw][:, 0:272].indirect(T.off[:, 0:8]), T[sr][:, 16:144], A.max, [rg(cw, 0, 272), rg("off", 0, 8), rg(sr, 16, 144)], [rg(sn, 16, 144)])
-        tw = turn(t + 1)
-        if t < 3:
-            in_order(T.fl[:, 0:16], [rg("fl", 0, 16)], tw, 288, 0)
-        fy = "fy%d" % t
-        in_order(T[fy][:, 0:16], [rg(fy, 0, 16)], tw, 288, 4)
-        if t < 3:
-            for a in range(1, 4):
-                dma("y", T[fy][32 * a:32 * a + 32, 0:16], T[fy][0:32, 0:16], [rg(fy, 0, 16, 0, 32)], [rg(fy, 0, 16, 32 * a, 32 * a + 32)])
-            tt(T.wr[:, 0:n], T.wr[:, 0:n], T.sq[:, 0:n], A.add, [rg("wr", 0, n), rg("sq", 0, n)], [rg("wr", 0, n)])
-            lift(0, n)
-        else:
-            for a in range(1, 4):
-                cp("v", fy, (0, 16), fy, (0, 16), (32 * a, 32 * a + 32), (0, 32))
-        if t == 0:
-            for o in range(O):
-                quantize("wt", 128 * o, 128, "wb")
-                mm("ps%d" % (5 + o), "wt", 128 * o, "w0", 0, P)
-            copy_slots("w0", "w1", 0, P)
-            copy_slots("w0", "w4", 0, 32)
-        elif t == 1:
-            pick_codes("qr", 384, "q", 128, "qoff", 24, 128)
-            for o, h in ((0, 1), (1, 0), (1, 1), (2, 0), (2, 1)):
-                y_gather("s", 0, o, h)
-        else:
-            if t == 3:
-                y_store(2, 0, 1)
-            for o, h in ((1, 1), (2, 0), (2, 1)):
-                y_gather("s", t - 1, o, h)
-            if t == 3:
-                y_store(2, 1, 3)
-        if t < 3:
-            if t == 0:
-                do("s", lambda: g.scalar.activation(T.wr[:, n:n + K], T.hq[:, 0:P].indirect(T.alst[:, 0:6]), AF.Copy), [rg("hq", 0, P), rg("alst", 0, 6)], [rg("wr", n, n + K)])
-                pick_codes("w1", n, "h", P, "alst", 0, K)
-                pick_scales("w1", n, "h", P, "alst", 0, K)
+            quantize("wt", 0, "wb")
+            for u in (2, 3):
+                iota(V("win%d" % u, 0, 128), [[0, 128]])
+            add_dma(3, 0, P)
+            mm_new(1, "qr", 128, 0)
+            square("u1", n, n + K, 1, 32)
+            lift(1, n, n + K)
+            quantize("wt", 128, "wb")
+        elif ahead:
+            if t == 1:
+                lift(2, 0, NS[1])
+                add(3, NS[0], NS[1])
+                y_gather("s", 0, 3, 4, 5)
             else:
-                mm("ps1", "qr", 128 * (t + 1), nx, n - 32, 128)
-                square("wr", n, "ps1", 32, K)
-            lift(n, n + K)
-            if t == 0:
-                for u in range(2, R):
-                    copy_slots("w0", "w%d" % u, 0, P)
-            for u in range(t + 2, R):
-                copy_slots(nx, "w%d" % u, n, n + K)
-            if t > 0:
-                y_store(t - 1, 0, O)
-        new_products(t)
-    new_copy(3, "s", 0)
-    y_gather("s", 3, 0, 0)
-    y_gather("v", 3, 0, 1)
-    new_copy(3, "v", 1)
-    new_copy(3, "s", 2)
-    y_gather("v", 3, 1, 0)
-    y_gather("s", 3, 1, 1)
-    y_gather("v", 3, 2, 0)
-    y_gather("s", 3, 2, 1)
+                lift(3, 160, NS[2])
+                y_gather("s", 1, 4, 5)
+            cp("v", V("bc", 0, K), (V("xa%d" % t, 0, 3), V("bl", 0, 6)))
+            tr(V("l%d" % (t + 1), n, n + K), V("bc", 0, K))
+        if ahead:
+            left("y", t)
+            y_store(t - 1, 0, O)
+        if t < 2:
+            copy_slots("w%d" % (t + 1), "w%d" % (t + 2), 0, n + K)
+    y_store(2, 0, 1)
+    y_gather("s", 2, 4)
+    y_gather("v", 2, 5)
+    left("y", 3)
+    y_store(2, 1, O)
+    new_products(3)
+    new_copy(3, "v", 0)
+    new_copy(3, "s", 1)
+    new_copy(3, "v", 2)
     for o in range(O):
+        y_gather("s", 3, 2 * o + 1)
+        y_gather("v", 3, 2 * o)
         y_store(3, o, o + 1)
 
     for sem in count:
-        if waited["g"].get(sem, 0) < count[sem]:
-            g.wait_ge(T.sem[sem], count[sem])
+        gate("g", sem)

@@ -1,46 +1,40 @@
-from concourse.bass import DstId, RemoteDMATransfer
 from concourse.mybir import dt, AluOpType as A, ActivationFunctionType as AF
 
 P, K, R, O = 256, 96, 4, 3
 PART = [1, 2, 4, 1]
 NS = [P + K * t for t in range(R + 1)]
 EPS = 2.0 ** -125
+TINY = 2.0 ** -100
 WIN = 1.0 - 2.0 ** -24
-AHEAD = (1, 2)
 
 SCRATCH = {"cb": ("sbuf", [128, 4 * P], "bfloat16"), "qb": ("sbuf", [128, 512], "bfloat16"), "wb": ("sbuf", [128, 512 * O], "bfloat16")}
-SEMAPHORES = ["sv", "ss", "st", "aq", "lq"] + ["d%d" % i for i in range(48)] + ["g%d" % i for i in range(40)]
-for _b, _n in (("q", 128), ("qr", 128 * R), ("qa", 16), ("qx", 128), ("wt", 128 * O)):
+SEMAPHORES = ["sv", "ss", "st"] + ["d%d" % i for i in range(32)] + ["g%d" % i for i in range(32)] + [k + "%d" % i for i in range(16) for k in "al"]
+for _b, _n in (("q", 128), ("qr", 128 * R), ("qa", 16), ("qx", 128), ("wt", 128 * O), ("h", P), ("out0", P), ("out2", K), ("out3", 2 * K),
+               ("w0", NS[0]), ("w2", NS[2]), ("w3", NS[3])):
     SCRATCH[_b + "c"] = ("sbuf", [128, _n], "float8_e4m3fn_x4")
     SCRATCH[_b + "s"] = ("sbuf", [128, _n], "uint8")
 for _t in range(R):
-    for _b, _n in (("w%d" % _t, NS[_t]), ("out%d" % _t, K if _t < 3 else 2 * K)):
-        SCRATCH[_b + "c"] = ("sbuf", [128, _n], "float8_e4m3fn_x4")
-        SCRATCH[_b + "s"] = ("sbuf", [128, _n], "uint8")
     SCRATCH["yb%d" % _t] = ("sbuf", [128, O * P], "float32")
     SCRATCH["u%d" % _t] = ("sbuf", [128, NS[_t]], "float32")
     SCRATCH["l%d" % _t] = ("sbuf", [128, NS[_t]], "float32")
-    SCRATCH["win%d" % _t] = ("sbuf", [128, 272], "bfloat16" if _t == 0 else "float32")
+    SCRATCH["win%d" % _t] = ("sbuf", [128, 288], "bfloat16" if _t < 2 else "float32")
     SCRATCH["lst%d" % _t] = ("sbuf", [128, 16], "uint16")
     SCRATCH["tab%d" % (_t + 1)] = ("sbuf", [128, 48], "uint16")
-    SCRATCH["xo%d" % _t] = ("sbuf", [128, 4], "float32")
-    SCRATCH["xa%d" % _t] = ("sbuf", [128, 4], "float32")
-    SEMAPHORES += ["ac%d" % _t, "as%d" % _t, "lc%d" % _t, "ls%d" % _t, "ax%d" % _t, "lx%d" % _t]
 SCRATCH["tab0"] = ("sbuf", [128, 48], "uint16")
 for _o in range(O):
     SCRATCH["yp%d" % _o] = ("sbuf", [128, NS[4]], "float32")
 for _b in range(8):
     SCRATCH["ps%d" % _b] = ("psum", [128, 512], "float32")
 for _b, _n in (("xs", NS[2]), ("u64", 64), ("t4", 64), ("rr", 128), ("rw", 128), ("mm", 128), ("pr", 128), ("col", 16), ("ci", 96), ("ct", 96),
-               ("cz", 160), ("ctr", 160), ("cw", 272), ("srow0", 64), ("srow1", 64), ("g1", 32), ("pay", 32), ("pf", 224), ("sa", 32), ("sb", 32),
-               ("z7", 8), ("gt", 96), ("bc", K), ("r3", 32)):
+               ("cz", 192), ("ctr", 192), ("cw", 272), ("rk", 272), ("srow0", 64), ("srow1", 64), ("g1", 32), ("pay", 32), ("pf", 384), ("sa", 48),
+               ("sb", 48), ("z7", 24), ("gt", 96), ("bc", K), ("r3", 32), ("x4", 32), ("zz", 32), ("b8", 8), ("hq", P), ("hx", P), ("xo", 4), ("xa", 4)):
     SCRATCH[_b] = ("sbuf", [128, _n], "float32")
-for _b, _n in (("c0", P), ("c1", P), ("kk", P), ("pb", 224)):
+for _b, _n in (("c0", P), ("c1", P), ("pb", 544)):
     SCRATCH[_b] = ("sbuf", [128, _n], "bfloat16")
-for _b, _n in (("qoff", 8 * R + 8), ("off", 2), ("co", 6), ("bl", 6)):
+for _b, _n in (("qoff", 8 * R + 8), ("kk", P), ("co", 8), ("alst", 8)):
     SCRATCH[_b] = ("sbuf", [128, _n], "uint16")
 FL, FY, UL, PL = 0, 16, 32, 36
-C_P, C_A, C_N, C_X, C_M, C_W, C_S, C_T = range(8)
+C_P, C_A, C_N, C_X, C_M, C_W, C_E = range(7)
 
 
 def rank_program(g, core, T, topo):
@@ -52,7 +46,7 @@ def rank_program(g, core, T, topo):
     count = {}
     waited = {q: {} for q in Q}
     recs = {}
-    used = {"d": 0, "g": 0}
+    used = {"d": 0, "g": 0, "a": 0, "l": 0}
 
     def V(b, c0, c1, step=1, p0=0, p1=128):
         return (b, c0, c1, step, p0, p1)
@@ -132,26 +126,22 @@ def rank_program(g, core, T, topo):
         count[sem] = 16
         note("y" if q == "y" else q + "d", sem, 16, reads, writes)
 
-    def send(t, o, i, sa, sl):
-        dst = T.cores[rank ^ PART[t]]
+    def send(x, o, i):
+        dst = T.cores[rank ^ x]
         rid, pid, _ = topo.addr(dst)
+        sa, sl = fresh("a"), fresh("l")
         need("g", [i], [])
         g.remote_dma(raw(o), raw(i), T.sem[sa], T.sem[sl], pid, rid, topo.mask(core, dst))
         count[sl] = len(topo.engines(core, dst))
         count[sa] = len(topo.engines(dst, core))
         note("r", sa, count[sa], [], [o])
+        return sl
+
+    def send_codes(x, ob, o0, ib, i0, n):
+        return [send(x, V(ob + k, o0, o0 + n), V(ib + k, i0, i0 + n)) for k in "cs"][0]
 
     def landing(t):
-        return ("w%d" % (t + 1), NS[t]) if t < 3 else ("out3", K)
-
-    def send_codes(t):
-        nx, n = landing(t)
-        for k in "cs":
-            send(t, V(nx + k, n, n + K), V("out%d%s" % (t, k), 0, K), "a%s%d" % (k, t), "l%s%d" % (k, t))
-
-    def left(q, t):
-        gate(q, "lc%d" % t)
-        gate(q, "ls%d" % t)
+        return (("w2", NS[0]), ("w2", NS[1]), ("w3", NS[2]), ("out3", K))[t]
 
     def cp(q, o, i):
         if q == "v":
@@ -159,6 +149,9 @@ def rank_program(g, core, T, topo):
             do("v", lambda: g.vector.tensor_copy(ap(o), ap(i)), [i] + ([o[1]] if len(o) == 2 else []), wr)
         else:
             do("s", lambda: g.scalar.activation(ap(o), ap(i), AF.Copy), [i], [o])
+
+    def act(o, i, func, bias=0.0, scale=1.0):
+        do("s", lambda: g.scalar.activation(ap(o), ap(i), func, bias=ap(bias), scale=scale), [i, bias], [o])
 
     def ts(o, i, s1, op0, s2=None, op1=None):
         if op1 is None:
@@ -176,10 +169,6 @@ def rank_program(g, core, T, topo):
         do("v", lambda: g.vector.transpose(ap(o), ap(i)), [i], [o])
 
     def iota(o, pattern, base=0, cm=0):
-        if o[5] - o[4] < 128 or used.get("part"):
-            for i in range(used["g"]):
-                gate("g", "g%d" % i)
-        used["part"] = o[5] - o[4] < 128
         do("g", lambda: g.iota(ap(o), pattern, base, cm, allow_small_or_imprecise_dtypes=True), [], [o])
 
     def pick_codes(ob, o0, ib, n, lst):
@@ -203,8 +192,7 @@ def rank_program(g, core, T, topo):
         do("v", lambda: g.vector.quantize_mx(ap(c), ap(s), ap(i)), [i], [c, s])
 
     def square(ob, c0, c1, bank, i0):
-        o, i = V(ob, c0, c1), V("ps%d" % bank, i0, i0 + c1 - c0)
-        do("s", lambda: g.scalar.activation(ap(o), ap(i), AF.Square), [i], [o])
+        act(V(ob, c0, c1), V("ps%d" % bank, i0, i0 + c1 - c0), AF.Square)
 
     def lift(t, c0, c1):
         ts(V("l%d" % t, c0, c1), V("u%d" % t, c0, c1), EPS, A.max)
@@ -216,9 +204,9 @@ def rank_program(g, core, T, topo):
         o, i = V("u%d" % t, c0, c1), V("u%d" % (t - 1), c0, c1)
         dma("g", ap(o), ap(i), [i, o], [o], add=True)
 
-    def copy_slots(frm, to, c0, c1):
+    def copy_slots(frm, to, c0, c1, shift=0):
         for k in "cs":
-            i, o = V(frm + k, c0, c1), V(to + k, c0, c1)
+            i, o = V(frm + k, c0, c1), V(to + k, c0 + shift, c1 + shift)
             dma("y", raw(o), raw(i), [i], [o])
 
     def col(k):
@@ -246,231 +234,248 @@ def rank_program(g, core, T, topo):
     dma("s", T.qb[:, 0:16], T.qt[:, 0:16], [], [V("qb", 0, 16)])
     for h in range(2):
         dma("y", T.cb[:, 512 * h:512 * h + 512], T.c[:, 512 * h:512 * h + 512], [], [V("cb", 512 * h, 512 * h + 512)])
-    dma("y", T.wb[:], T.w[:], [V("cb", 0, 4 * P)], [V("wb", 0, 512 * O)])
+    for o in range(O):
+        dma("y", T.wb[:, 512 * o:512 * o + 512], T.w[:, 512 * o:512 * o + 512], [V("cb", 0, 4 * P)], [V("wb", 512 * o, 512 * o + 512)])
+    iota(V("b8", 0, 8), [[1, 2], [0, 4]])
+    iota(V("x4", 0, 32), [[0, 8], [4, 4]])
     iota(V("ci", 0, 32), [[128, 2], [0, 16]])
     iota(V("ci", 32, 64), [[0, 2], [2, 16]])
     iota(V("ci", 64, 96), [[1, 32]])
     iota(col(C_P), [[0, 1]], 0, 1)
     iota(V("pr", 0, 128), [[1, 2], [32, 4], [2, 16]])
     fill(V("qb", 16, 512), 0.0)
-    for t in range(R):
-        fill(qlist(t), t)
-    fill(V("cz", 0, 128), 0.0)
+    fill(qlist(0), 0)
+    for s in range(2):
+        fill(V("srow%d" % s, 0, 64), 0.0)
+    fill(V("cz", 64, 160), 0.0)
     fill(V("cw", 0, 272), -2000.0)
     tr(V("ct", 0, 96), V("ci", 0, 96))
-    fill(V("win0", 0, 128), 0.0)
+    fill(V("win0", 0, 288), 0.0)
+    fill(col(C_E), TINY)
     ts(col(C_A), col(C_P), I1, A.subtract)
     ts(col(C_N), H128, -1.0, A.mult, 128.0, A.add)
     ts(col(C_M), Q2, 16.0, A.is_lt)
     ts(col(C_X), Q2, col(C_A), A.add)
     ts(col(C_W), col(C_N), 1.0 / 128, A.mult, WIN, A.max)
-    for s in range(2):
-        fill(V("srow%d" % s, 0, 64), 0.0)
+    iota(V("cz", 96, 112), [[1, 8], [9, 2]])
+    iota(V("cz", 112, 128), [[1, 8], [-8, 2]], 8)
     iota(V("r3", 0, 32), [[1, 2], [2, 16]])
-    iota(V("cz", 96, 102), [[1, 3], [4, 2]])
-    iota(V("cz", 112, 118), [[1, 3], [-3, 2]], 3)
     iota(V("cw", 16, 16 + K), [[1, K]])
-
-    quantize("q", 0, "qb")
-    ts(V("tab0", FL, FL + 8), V("pr", 0, 128, 16), Q2, A.add, H128, A.add)
-    for t in range(2):
-        pick_codes("qr", 128 * t, "q", 128, qlist(t))
-    for t in range(3):
-        pick_scales("qr", 128 * t, "q", 128, qlist(t))
-    need("g", [V("qc", 0, 128), V("qs", 0, 128)], [])
-    for k in "cs":
-        trs = []
-        for j, t in enumerate(AHEAD):
-            dst = T.cores[rank ^ PART[t]]
-            rid, pid, _ = topo.addr(dst)
-            es = topo.engines(core, dst)
-            es = es[j * len(es) // 2:(j + 1) * len(es) // 2]
-            trs.append(RemoteDMATransfer(dst_ids=[DstId(rid=rid, pnc=pid)], dma_engine_mask=sum(1 << e for e in es), remote_sem=T.sem.aq,
-                                         src=raw(V("q" + k, t + 1, t + 3)), dst=raw(V("qa" + k, 2 * j, 2 * j + 2))))
-            count["lq"] = count.get("lq", 0) + len(es)
-            count["aq"] = count.get("aq", 0) + len(topo.engines(dst, core)) // 2
-        g.remote_dma_fused(trs, local_sem=T.sem.lq)
-    note("r", "aq", count["aq"], [], [V("qac", 0, 4), V("qas", 0, 4)])
-    iota(V("cz", 0, 16), [[16, 2], [64, 2], [0, 4]])
-    iota(V("cz", 16, 32), [[-16, 2], [-32, 2], [0, 4]], 48)
-    iota(V("cz", 32, 48), [[64, 2], [16, 2], [0, 4]])
-    iota(V("cz", 48, 64), [[-32, 2], [16, 2], [0, 4]], 32)
-    iota(V("cz", 64, 68), [[64, 2], [16, 2]])
-    iota(V("cz", 68, 70), [[64, 2]])
-    iota(V("cz", 84, 86), [[-32, 2]], 48)
+    for j, (b, x, y) in enumerate(((0, 16, 64), (48, -16, -32), (0, 64, 16), (32, -32, 16))):
+        for i in range(2):
+            act(V("cz", 16 * j + 8 * i, 16 * j + 8 * i + 8), V("b8", 0, 8), AF.Identity, float(b + x * i), float(y))
+    cp("s", V("cz", 64, 68), V("cz", 32, 48, 4))
+    cp("s", V("cz", 68, 70), V("cz", 32, 48, 8))
+    cp("s", V("cz", 84, 86), V("cz", 16, 24, 4))
     for a in range(4):
-        iota(V("cz", 128, 160, 1, 32 * a, 32 * a + 32), [[0, 8], [8 - 16 * (a // 2), 2], [4 - 8 * (a % 2), 2]], 4 * a)
-    iota(V("win1", 0, 128), [[0, 128]])
+        for e in range(2):
+            x, p = e ^ (a in (1, 2)), 32 * a
+            act(V("cz", 160 + e, 192, 2, p, p + 32), V("x4", x, 32, 2, p, p + 32), AF.Identity, 12.0 * (a // 2), 1.0 - 2 * (a // 2))
 
-    quantize("w0", 0, "cb")
-    mm(0, "qr", 0, "w0", 0, 128)
-    square("u0", 0, 128, 0, 0)
-    pick_scales("qr", 384, "q", 128, qlist(3))
+    ts(V("tab0", FL, FL + 8), V("pr", 0, 128, 16), Q2, A.add, H128, A.add)
     ts(V("tab0", FL + 8, FL + 16), V("pr", 0, 128, 16), Q2, A.add, col(C_N), A.add)
     for h in range(2):
         ts(V("tab0", UL + h, UL + 4, 2), V("pr", 0, 128, 64), col(C_X), A.add, 128.0 * h, A.add)
     ts(V("mm", 0, 128), V("pr", 0, 128), col(C_X), A.is_gt, WIN, A.max)
+
+    quantize("q", 0, "qb")
+    for t in (1, 2):
+        fill(qlist(t), t)
+    pick_codes("qr", 0, "q", 128, qlist(0))
+    for t in range(2):
+        pick_scales("qr", 128 * t, "q", 128, qlist(t))
+    send_codes(PART[2], "qa", 0, "q", 3, 2)
+
+    quantize("w0", 0, "cb")
+    mm(0, "qr", 0, "w0", 0, 128)
+    act(V("l0", 0, 128), V("ps0", 0, 128), AF.Abs, col(C_E))
+    fill(qlist(3), 3)
     quantize("w0", 128, "cb")
     mm(1, "qr", 0, "w0", 128, 128)
-    square("u0", 128, 256, 1, 0)
-    pick_codes("qr", 256, "q", 128, qlist(2))
-    mm(6, "qr", 128, "w0", 0, P)
-    mm(7, "qr", 256, "w0", 0, P)
-    lift(0, 0, 128)
-    ts(col(C_S), Q2, 16.0, A.is_ge, -3.0, A.mult)
-    lift(0, 128, 256)
+    act(V("l0", 128, 256), V("ps1", 0, 128), AF.Abs, col(C_E))
+    for t in (1, 2):
+        pick_codes("qr", 128 * t, "q", 128, qlist(t))
+    mm(5, "qr", 128, "w0", 0, P)
+    copy_slots("w0", "w2", 0, P)
+    for u in (1, 2, 3):
+        iota(V("win%d" % u, 0, 128), [[0, 128]])
+    iota(V("zz", 0, 32), [[0, 32]])
 
     for t in range(R):
         n, tab, nt = NS[t], "tab%d" % t, "tab%d" % (t + 1)
         lw, wn, ls = V("l%d" % t, 0, n), "win%d" % t, "lst%d" % t
         sr, sn = "srow%d" % (t % 2), "srow%d" % ((t + 1) % 2)
-        pp = "pb" if t == 0 else "pf"
-        off = V("off", 0, 2)
-        ahead = t in AHEAD
+        pp = "pb" if t < 2 else "pf"
+        off = V("kk", P - 2, P)
+        alst = V("alst", 0, 6)
         cp("s", V("u64", 0, 64), (lw, V(tab, UL, UL + 4)))
         cp("s", V("rw", 0, 128), (lw, V(tab, FL + 8, FL + 16)))
         tt(V("rr", 0, 128), (lw, V(tab, FL, FL + 8)), V("mm", 0, 128), A.mult)
         tr(V("t4", 0, 64), V("u64", 0, 64))
         if t == 0:
-            square("u1", 0, P, 6, 0)
-            square("u2", 0, P, 7, 0)
+            for h in range(2):
+                square("u0", 128 * h, 128 * h + 128, h, 0)
+            square("u1", 0, P, 5, 0)
+            for u in (2, 3):
+                pick_scales("qr", 128 * u, "q", 128, qlist(u))
+            mm(6, "qr", 256, "w0", 0, P)
+            square("u2", 0, P, 6, 0)
+            for h in range(2):
+                for e in range(2):
+                    act(V("cz", 128 + 16 * h + e, 134 + 16 * h, 2), V("cz", 96 + 16 * h + e, 102 + 16 * h, 2), AF.Identity, -5.0 * (e != h))
+            for c in (0, 16 + K, 16 + 2 * K):
+                w = min(16 + K, 272 - c) if c == 0 else min(K, 272 - c)
+                act(V("rk", c, c + w), V("cw", min(c, 16), min(c, 16) + w), AF.Identity, float(max(c - 16, 0)))
             ts(V("g1", 0, 32), V("r3", 0, 32), H128, A.add, col(C_A), A.add)
+            tr(V("ctr", 96, 128), V("cz", 96, 128))
         if t == 1:
-            quantize("wt", 256, "wb")
-        if ahead:
-            mm_new(0, "qx", 0, t - 1)
-            mm_new(1, "qr", 256, t - 1)
-            square("xs", NS[t - 1], n, 0, 32)
-            for o in range(O if t == 1 else 0):
-                mm(5 + o, "wt", 128 * o, "w0", 0, P)
-            mm_new(0, "qr", 384, t - 1)
-            new_products(t - 1)
-            square("u2", NS[t - 1], n, 1, 32)
-            square("u3", NS[t - 1], n, 0, 32)
-        if t == 1:
-            for o in range(O):
-                cp("s", V("yp%d" % o, 0, P), V("ps%d" % (5 + o), 0, P))
+            lift(2, 0, 80)
         if t == 2:
-            lift(3, 0, 80)
-        if t == 3:
-            new_products(2)
-        if t > 0:
+            pick_codes("w2", NS[1], "h", P, V("alst", 0, 4))
+            cp("s", V("xs", NS[1], n), (V("hx", 0, P), alst))
+            pick_scales("w2", NS[1], "h", P, V("alst", 0, 4))
+            pick_scales("w2", NS[1] + 64, "h", P, V("alst", 4, 6))
+
+        def beside():
+            new_products(t - 1)
+            if t < 3:
+                mm_new(1, "qr", 256, t - 1)
+            if t == 1:
+                mm(0, "qr", 384, "w2", 0, n)
+            if t == 2:
+                mm_new(0, "qr", 384, 1)
             for o in range(O):
                 new_copy(t - 1, "s", o)
-            y_gather("s", t - 1, *range(3 if t == 1 else 4))
+            if t < 3:
+                square("u2", NS[t - 1], n, 1, 32)
+                square("u3", NS[1] * (t - 1), n, 0, 32 * (t - 1))
+            if t == 1:
+                pick_scales("qx", 0, "qa", 2, qlist(4))
+            y_gather("s", t - 1, *range((5, 3, 4)[t - 1]))
+        if t == 3:
+            y_gather("s", 1, 5)
+            gate("y", left)
+            y_store(1, 0, O)
+        if t in (1, 3):
+            beside()
+        if t == 3:
+            y_store(2, 0, 1)
         for e in range(2):
             ts(V("c%d" % e, 0, 128), V("rr", 0, 128), V("t4", 32 * e, 32 * e + 1), A.is_lt)
         for e in range(2):
             ts(V("c%d" % e, 128, 256), V("rw", 0, 128), col(C_W), A.mult, V("t4", 32 * e, 32 * e + 1), A.is_lt)
-        for e in range(2):
-            a, b, o = V("c%d" % e, 0, 128), V("c%d" % e, 128, 256), V("kk", 128 * e, 128 * e + 128)
-            do("v", lambda: g.vector.tensor_tensor_scan(ap(o), ap(a), ap(b), float(e - 1), A.add, A.add), [a, b], [o])
         if t == 0:
             ts(V(sr, 16, 48), V("g1", 0, 32), col(C_M), A.mult, EPS, A.max)
-        if t == 1:
-            tt(V("pay", 0, 32), (V("xs", 0, n), V(tab, PL, PL + 2)), V(sr, 16, 48), A.max)
         if t == 2:
-            lift(3, 80, 160)
-        ts(off, V("kk", 127, 256, 128), 16.0, A.add)
+            tt(V("pay", 0, 32), (V("xs", 0, n), V(tab, PL, PL + 2)), V(sr, 16, 48), A.max)
+        for e in range(2):
+            a, b, o = V("c%d" % e, 0, 128), V("c%d" % e, 128, 256), V("kk", e, P, 2)
+            do("v", lambda: g.vector.tensor_tensor_scan(ap(o), ap(a), ap(b), float(e + 15), A.add, A.add), [a, b], [o])
         if t == 0:
-            tr(V("ctr", 96, 128), V("cz", 96, 128))
+            cp("v", V("co", 4, 5), V("ctr", 96, 97))
         if t == 1:
-            fill(V("bl", 2, 4), 1)
+            lift(2, 80, 160)
         if t == 2:
-            tt(V("pay", 0, 32), (V("xs", 0, n), V(tab, PL, PL + 2)), V(sr, 16, 48), A.max)
-        cp("v", (V(wn, 0, 272), off), V("pay", 0, 32) if ahead else V(sr, 16, 48))
+            pick_codes("w2", NS[1] + 64, "h", P, V("alst", 4, 6))
+            copy_slots("w2", "w3", NS[1], n)
+            beside()
+        cp("v", (V(wn, 0, 272), off), V("pay", 0, 32) if t in (1, 2) else V(sr, 16, 48))
         ts(V("g1", 0, 32), (V("cw", 0, 272), off), float(n), A.add, col(C_M), A.mult)
-        tr(V(pp, 0, 96), V(wn, 16, 112))
-        tr(V(pp, 96, 224), V(wn, 0, 128))
+        k = P if t == 0 else K
+        tr(V(pp, 0, k), V(wn, 16, 16 + k))
+        tr(V(pp, k, 2 * k + 32), V(wn, 0, 32 + k))
         tt(V(sn, 16, 48), V("g1", 0, 32), V(sr, 16, 48), A.max)
-        r0, st = (4 * (t - 1), 8) if ahead else (0, 16)
-        m = 224 // st
-        tt(V("sa", 0, m, 1, 0, 64), V(pp, r0, 224, st, 0, 64), V(pp, r0, 224, st, 64, 128), A.add)
+        st = 8 if t == 2 else 16
+        m = (2 * k + 32) // st
+        tt(V("sa", 0, m, 1, 0, 64), V(pp, 0, m * st, st, 0, 64), V(pp, 0, m * st, st, 64, 128), A.add)
         tr(V("gt", 0, 32), V(sn, 16, 48))
         for p in (0, 32):
             tt(V("sb", 0, m, 1, p, p + 32), V("sa", 0, m, 1, 0, 32), V("sa", 0, m, 1, 32, 64), A.add)
         tr(V("gt", 32, 96), V(sn, 0, 64))
-        if ahead:
-            for p in (0, 64):
-                tt(V("xo%d" % t, 0, 3, 1, p, p + 64), V("sb", 1, 12, 4, 0, 64), V("sb", 3, 12, 4, 0, 64), A.add)
-            send(t, V("xa%d" % t, 0, 3), V("xo%d" % t, 0, 3), "ax%d" % t, "lx%d" % t)
-        s2 = 4 if ahead else 2
-        for p in (0, 64):
-            tt(V("z7", 0, 7, 1, p, p + 64), V("sb", 0, m, s2, 0, 64), V("sb", s2 // 2, m, s2, 0, 64), A.add)
-        if t == 0:
-            cp("v", V("co", 4, 5), V("ctr", 96, 97))
-        else:
-            cp("v", V("gt", 8, 96, 16, 0, 64), V("gt", 0, 96, 16, 64, 128))
-        cp("v", V(ls, 0, 16), (V("z7", 0, 7), V("co", 4, 5)))
-        if t == 0:
-            cp("v", V("gt", 8, 96, 16, 0, 64), V("gt", 0, 96, 16, 64, 128))
-        cp("s", V("gt", 8, 96, 16, 64, 128), V("gt", 0, 96, 16, 0, 64))
-        if t > 0:
-            cp("v", V("gt", 4, 96, 8, 0, 32), V("gt", 0, 96, 8, 32, 64))
-        pick_codes("out%d" % t, 0, "w%d" % t, n, V(ls, 0, 6))
-        pick_scales("out%d" % t, 0, "w%d" % t, n, V(ls, 0, 6))
-        send_codes(t)
-
-        if t == 0:
-            cp("v", V("gt", 4, 96, 8, 0, 32), V("gt", 0, 96, 8, 32, 64))
-        cp("v", V("gt", 4, 96, 8, 32, 64), V("gt", 0, 96, 8, 0, 32))
-        cp("s", V("gt", 4, 96, 8, 64, 96), V("gt", 0, 96, 8, 96, 128))
-        cp("s", V("gt", 4, 96, 8, 96, 128), V("gt", 0, 96, 8, 64, 96))
-        if t == 0:
-            ts(col(C_T), Q2, 24.0, A.is_ge, 2.0, A.mult)
-            quantize("w1", 128, "cb")
-            add(1, 0, P)
-            add_dma(2, 0, P)
-            ts(qlist(4), qlist(3), col(C_S), A.add, col(C_T), A.add)
-            pick_codes("qr", 384, "q", 128, qlist(3))
-            mm(0, "qr", 384, "w0", 0, P)
-            pick_scales("qx", 0, "qa", 4, qlist(4))
-            pick_codes("qx", 0, "qa", 4, qlist(4))
-            mm(2, "qx", 0, "w0", 0, P)
-            square("u3", 0, P, 0, 0)
-            square("xs", 0, P, 2, 0)
-            tr(V("ctr", 0, 96), V("cz", 0, 96))
-            tr(V("ctr", 128, 160), V("cz", 128, 160))
-            lift(1, 0, P)
-            ts(V("co", 0, 2), V("ctr", 0, 64, 32), V("ctr", 128, 129), A.add)
-            cp("v", V("co", 2, 3), V("ctr", 64, 65))
-            quantize("w1", 0, "cb")
-        if t == 1:
-            add(2, NS[0], NS[1])
-            fill(V("bl", 0, 2), 0)
-            fill(V("bl", 4, 6), 2)
         if t == 2:
-            add(3, NS[1], NS[2])
-        cp("v", V(nt, 0, 48), (V("gt", 0, 96), V("co", 0, 3)))
+            for p in (0, 64):
+                tt(V("xo", 0, 3, 1, p, p + 64), V("sb", 1, 12, 4, 0, 64), V("sb", 3, 12, 4, 0, 64), A.add)
+            send(PART[t], V("xa", 0, 3), V("xo", 0, 3))
+        s2 = 32 // st
+        for p in (0, 64):
+            tt(V("z7", 0, m // s2, 1, p, p + 64), V("sb", 0, m, s2, 0, 64), V("sb", s2 // 2, m, s2, 0, 64), A.add)
         if t == 0:
             quantize("wt", 0, "wb")
-            for u in (2, 3):
-                iota(V("win%d" % u, 0, 128), [[0, 128]])
-            add_dma(3, 0, P)
+        elif t < 3:
+            lift(t + 1, 160 * (t == 1), 160 * (t == 1) + 96)
+        cp("v", V(ls, 0, 16), (V("z7", 0, m // s2), V("co", 6, 7) if t else V("co", 4, 5)))
+        if t == 0:
+            quantize("wt", 128, "wb")
+        if t == 2:
+            lift(3, 96, 192)
+        if t == 1:
+            left = send(PART[t], alst, V(ls, 0, 6))
+        else:
+            pick_codes("out%d" % t, 0, "w%d" % t, n, V(ls, 0, 6))
+            pick_scales("out%d" % t, 0, "w%d" % t, n, V(ls, 0, 6))
+            left = send_codes(PART[t], *landing(t), "out%d" % t, 0, K)
+        if t == 0:
+            pick_codes("out0", K, "w0", n, V(ls, 6, 16))
+            pick_scales("out0", K, "w0", n, V(ls, 6, 16))
+            send_codes(PART[1], "h", K, "out0", K, P - K)
+            send_codes(PART[0] ^ PART[1], "h", 0, "out0", 0, K)
+
+        if t == 3:
+            y_gather("s", 2, 4)
+            y_gather("v", 2, 5)
+            y_store(2, 1, O)
+        for p in (0, 64):
+            cp("s", V("gt", 8, 96, 16, p, p + 64), V("gt", 0, 96, 16, 64 - p, 128 - p))
+        for p in range(0, 128, 32):
+            cp("s", V("gt", 4, 96, 8, p, p + 32), V("gt", 0, 96, 8, p ^ 32, (p ^ 32) + 32))
+        if t == 0:
+            cp("s", V("pay", 0, 32), (V("rk", 0, 272), off))
+            quantize("wt", 256, "wb")
+            for o in range(O):
+                mm(5 + o, "wt", 128 * o, "w0", 0, P)
+                cp("s", V("yp%d" % o, 0, P), V("ps%d" % (5 + o), 0, P))
+            tr(V("ctr", 0, 96), V("cz", 0, 96))
+            tr(V("ctr", 128, 192), V("cz", 128, 192))
+            add(1, 0, P)
+            ts(V("co", 0, 2), V("ctr", 0, 64, 32), V("ctr", 160, 161), A.add)
+            cp("v", V("co", 2, 7, 4), V("ctr", 64, 129, 64))
+            lift(1, 0, P)
+        if t == 1:
+            pick_codes("qx", 0, "qa", 2, qlist(4))
+            add(2, NS[0], NS[1])
+        if t == 2:
+            add(3, P, n)
+        cp("v", V(nt, 0, 48), (V("gt", 0, 96), V("co", 0, 3)))
+        if t == 0:
+            ts(qlist(4), qlist(0), col(C_M), A.add)
+            add(2, 0, P)
+            pick_codes("qr", 384, "q", 128, qlist(3))
             mm_new(1, "qr", 128, 0)
             square("u1", n, n + K, 1, 32)
             lift(1, n, n + K)
-            quantize("wt", 128, "wb")
-        elif ahead:
-            if t == 1:
-                lift(2, 0, NS[1])
-                add(3, NS[0], NS[1])
-                y_gather("s", 0, 3, 4, 5)
-            else:
-                lift(3, 160, NS[2])
-                y_gather("s", 1, 4, 5)
-            cp("v", V("bc", 0, K), (V("xa%d" % t, 0, 3), V("bl", 0, 6)))
-            tr(V("l%d" % (t + 1), n, n + K), V("bc", 0, K))
-        if ahead:
-            left("y", t)
-            y_store(t - 1, 0, O)
-        if t < 2:
-            copy_slots("w%d" % (t + 1), "w%d" % (t + 2), 0, n + K)
-    y_store(2, 0, 1)
-    y_gather("s", 2, 4)
-    y_gather("v", 2, 5)
-    left("y", 3)
-    y_store(2, 1, O)
+        if t == 1:
+            need("y", [V(ls, 0, 6)], [])
+            copy_slots("w2", "w3", 0, n)
+            mm(1, "qr", 256, "h", K, P - K)
+            mm(0, "qx", 0, "w2", 0, n)
+            mm(2, "qr", 256, "h", 0, 128)
+            mm(5, "qx", 0, "h", 0, P)
+            square("hq", K, P, 1, 0)
+            square("xs", 0, n, 0, 0)
+            square("hq", 0, K, 2, 0)
+            square("hx", 0, P, 5, 0)
+            lift(2, P, NS[1])
+            y_gather("v", 0, 5)
+            y_store(0, 0, O)
+            add(3, 0, P)
+            ts(V("l2", n, n + K), (V("hq", 0, P), alst), EPS, A.max)
+        if t == 2:
+            y_gather("s", 1, 3, 4)
+            lift(3, 192, n)
+            for j in range(2):
+                ts(V("bc", 32 * j, 32 * j + 32), V("zz", 0, 32), V("xa", j, j + 1), A.add)
+            act(V("bc", 64, K), V("zz", 0, 32), AF.Identity, V("xa", 2, 3))
+            tr(V("l3", n, n + K), V("bc", 0, K))
     new_products(3)
     new_copy(3, "v", 0)
     new_copy(3, "s", 1)

from concourse.mybir import dt, AluOpType as A, ActivationFunctionType as AF

P, K, R, O = 256, 96, 4, 3
PART = [1, 2, 4, 1]
NS = [P + K * t for t in range(R + 1)]
EPS = 2.0 ** -125
TINY = 2.0 ** -100
WIN = 1.0 - 2.0 ** -24

SCRATCH = {"cb": ("sbuf", [128, 4 * P], "bfloat16"), "qb": ("sbuf", [128, 512], "bfloat16"), "wb": ("sbuf", [128, 512 * O], "bfloat16")}
SEMAPHORES = ["sv", "ss", "st"] + ["d%d" % i for i in range(32)] + ["g%d" % i for i in range(32)] + [k + "%d" % i for i in range(16) for k in "al"]
for _b, _n in (("q", 128), ("qr", 128 * R), ("qa", 16), ("qx", 128), ("wt", 128 * O), ("h", P), ("out0", P), ("out2", K), ("out3", 2 * K),
               ("w0", NS[0]), ("w2", NS[2]), ("w3", NS[3])):
    SCRATCH[_b + "c"] = ("sbuf", [128, _n], "float8_e4m3fn_x4")
    SCRATCH[_b + "s"] = ("sbuf", [128, _n], "uint8")
for _t in range(R):
    SCRATCH["yb%d" % _t] = ("sbuf", [128, O * P], "float32")
    SCRATCH["u%d" % _t] = ("sbuf", [128, NS[_t]], "float32")
    SCRATCH["l%d" % _t] = ("sbuf", [128, NS[_t]], "float32")
    SCRATCH["win%d" % _t] = ("sbuf", [128, 288], "bfloat16" if _t < 2 else "float32")
    SCRATCH["lst%d" % _t] = ("sbuf", [128, 16], "uint16")
    SCRATCH["tab%d" % (_t + 1)] = ("sbuf", [128, 48], "uint16")
SCRATCH["tab0"] = ("sbuf", [128, 48], "uint16")
for _o in range(O):
    SCRATCH["yp%d" % _o] = ("sbuf", [128, NS[4]], "float32")
for _b in range(8):
    SCRATCH["ps%d" % _b] = ("psum", [128, 512], "float32")
for _b, _n in (("xs", NS[2]), ("u64", 64), ("t4", 64), ("rr", 128), ("rw", 128), ("mm", 128), ("pr", 128), ("col", 16), ("ci", 96), ("ct", 96),
               ("cz", 192), ("ctr", 192), ("cw", 272), ("rk", 272), ("srow0", 64), ("srow1", 64), ("g1", 32), ("pay", 32), ("pf", 384), ("sa", 48),
               ("sb", 48), ("z7", 24), ("gt", 96), ("bc", K), ("r3", 32), ("x4", 32), ("zz", 32), ("b8", 8), ("hq", P), ("hx", P), ("xo", 4), ("xa", 4)):
    SCRATCH[_b] = ("sbuf", [128, _n], "float32")
for _b, _n in (("c0", P), ("c1", P), ("pb", 544)):
    SCRATCH[_b] = ("sbuf", [128, _n], "bfloat16")
for _b, _n in (("qoff", 8 * R + 8), ("kk", P), ("co", 8), ("alst", 8)):
    SCRATCH[_b] = ("sbuf", [128, _n], "uint16")
FL, FY, UL, PL = 0, 16, 32, 36
C_P, C_A, C_N, C_X, C_M, C_W, C_E = range(7)


def rank_program(g, core, T, topo):
    rank = T.rank_of(core)
    if rank is None:
        return
    Q = {"g": g, "v": g.vector, "s": g.scalar, "t": g.tensor, "y": g.sync}
    own = {"v": "sv", "s": "ss", "t": "st"}
    count = {}
    waited = {q: {} for q in Q}
    recs = {}
    used = {"d": 0, "g": 0, "a": 0, "l": 0}

    def V(b, c0, c1, step=1, p0=0, p1=128):
        return (b, c0, c1, step, p0, p1)

    def ap(r):
        if not isinstance(r, tuple):
            return r
        if len(r) == 2:
            return ap(r[0]).indirect(ap(r[1]))
        return T[r[0]][r[4]:r[5], r[1]:r[2]:r[3]] if r[3] > 1 else T[r[0]][r[4]:r[5], r[1]:r[2]]

    def flat(rs):
        out = []
        for r in rs:
            if isinstance(r, tuple):
                out += list(r) if len(r) == 2 else [r]
        return out

    def cols(r):
        return set(range(r[1], r[2], r[3]))

    def meets(a, b):
        return a[0][:2] == "ps" or (a[4] < b[5] and b[4] < a[5] and len(cols(a) & cols(b)) > 0)

    def covers(a, b):
        return a[0][:2] == "ps" or (a[4] <= b[4] and a[5] >= b[5] and cols(b) <= cols(a))

    def gate(q, sem, n=None):
        n = n or count[sem]
        if waited[q].get(sem, 0) < n:
            Q[q].wait_ge(T.sem[sem], n)
            waited[q][sem] = n

    def need(q, reads, writes):
        w = {}
        for regs, wr in ((reads, False), (writes, True)):
            for r in regs:
                for (x, xq, sem, n, xw) in recs.get(r[0], []):
                    if not (wr or xw) or not meets(r, x):
                        continue
                    if wr and not xw and xq == q and q not in "yg":
                        continue
                    if r[0][:2] == "ps" and xq == q:
                        continue
                    w[sem] = max(w.get(sem, 0), n)
        for sem in w:
            gate(q, sem, w[sem])

    def note(q, sem, n, reads, writes):
        for r in writes:
            recs[r[0]] = [e for e in recs.get(r[0], []) if not covers(r, e[0])]
        for r in writes:
            recs.setdefault(r[0], []).append((r, q, sem, n, True))
        for r in reads:
            recs.setdefault(r[0], []).append((r, q, sem, n, r[0][:2] == "ps"))

    def fresh(kind):
        used[kind] += 1
        return "%s%d" % (kind, used[kind] - 1)

    def do(q, call, reads, writes):
        reads = flat(reads)
        need(q, reads, writes)
        sem = own[q] if q in own else fresh("g")
        count[sem] = count.get(sem, 0) + 1
        call().then_inc(T.sem[sem], 1)
        note(q, sem, count[sem], reads, writes)

    def raw(r):
        return ap(r).bitcast(dt.uint8) if SCRATCH[r[0]][2] == "float8_e4m3fn_x4" else ap(r)

    def dma(q, out, in_, reads, writes, add=False):
        need(q, reads, writes)
        sem = fresh("d")
        ins = g.dma_start(out, in_, accum_op=A.add) if add else Q[q].dma_start(out, in_)
        ins.then_inc(T.sem[sem], 16)
        count[sem] = 16
        note("y" if q == "y" else q + "d", sem, 16, reads, writes)

    def send(x, o, i):
        dst = T.cores[rank ^ x]
        rid, pid, _ = topo.addr(dst)
        sa, sl = fresh("a"), fresh("l")
        need("g", [i], [])
        g.remote_dma(raw(o), raw(i), T.sem[sa], T.sem[sl], pid, rid, topo.mask(core, dst))
        count[sl] = len(topo.engines(core, dst))
        count[sa] = len(topo.engines(dst, core))
        note("r", sa, count[sa], [], [o])
        return sl

    def send_codes(x, ob, o0, ib, i0, n):
        return [send(x, V(ob + k, o0, o0 + n), V(ib + k, i0, i0 + n)) for k in "cs"][0]

    def landing(t):
        return (("w2", NS[0]), ("w2", NS[1]), ("w3", NS[2]), ("out3", K))[t]

    def cp(q, o, i):
        if q == "v":
            wr = [o[0]] if len(o) == 2 else [o]
            do("v", lambda: g.vector.tensor_copy(ap(o), ap(i)), [i] + ([o[1]] if len(o) == 2 else []), wr)
        else:
            do("s", lambda: g.scalar.activation(ap(o), ap(i), AF.Copy), [i], [o])

    def act(o, i, func, bias=0.0, scale=1.0):
        do("s", lambda: g.scalar.activation(ap(o), ap(i), func, bias=ap(bias), scale=scale), [i, bias], [o])

    def ts(o, i, s1, op0, s2=None, op1=None):
        if op1 is None:
            do("v", lambda: g.vector.tensor_scalar(ap(o), ap(i), ap(s1), None, op0), [i, s1], [o])
        else:
            do("v", lambda: g.vector.tensor_scalar(ap(o), ap(i), ap(s1), ap(s2), op0, op1), [i, s1, s2], [o])

    def tt(o, a, b, op):
        do("v", lambda: g.vector.tensor_tensor(ap(o), ap(a), ap(b), op), [a, b], [o])

    def fill(o, v):
        do("v", lambda: g.vector.memset(ap(o), v), [], [o])

    def tr(o, i):
        do("v", lambda: g.vector.transpose(ap(o), ap(i)), [i], [o])

    def iota(o, pattern, base=0, cm=0):
        do("g", lambda: g.iota(ap(o), pattern, base, cm, allow_small_or_imprecise_dtypes=True), [], [o])

    def pick_codes(ob, o0, ib, n, lst):
        o, i = V(ob + "c", o0, o0 + 16 * (lst[2] - lst[1])), V(ib + "c", 0, n)
        do("v", lambda: g.vector.tensor_copy(ap(o).bitcast(dt.uint32), ap(i).bitcast(dt.uint32).indirect(ap(lst))), [i, lst], [o])

    def pick_scales(ob, o0, ib, n, lst):
        cp("s", V(ob + "s", o0, o0 + 16 * (lst[2] - lst[1])), (V(ib + "s", 0, n), lst))

    def mm(bank, lc, l0, rc, r0, n):
        ins = [V(lc + "c", l0, l0 + 128), V(lc + "s", l0, l0 + 128), V(rc + "c", r0, r0 + n), V(rc + "s", r0, r0 + n)]
        b = "ps%d" % bank
        do("t", lambda: g.tensor.matmul_mx(T[b][:, 0:n], ap(ins[0]), ap(ins[1]), ap(ins[2]), ap(ins[3]), True, True), ins, [V(b, 0, 512)])

    def mm_new(bank, lc, l0, t):
        nx, n = landing(t)
        mm(bank, lc, l0, nx, n - 32, 128)

    def quantize(ob, o0, ib):
        c, s, i = V(ob + "c", o0, o0 + 128), V(ob + "s", o0, o0 + 128), V(ib, 4 * o0, 4 * o0 + 512)
        do("v", lambda: g.vector.quantize_mx(ap(c), ap(s), ap(i)), [i], [c, s])

    def square(ob, c0, c1, bank, i0):
        act(V(ob, c0, c1), V("ps%d" % bank, i0, i0 + c1 - c0), AF.Square)

    def lift(t, c0, c1):
        ts(V("l%d" % t, c0, c1), V("u%d" % t, c0, c1), EPS, A.max)

    def add(t, c0, c1):
        tt(V("u%d" % t, c0, c1), V("u%d" % t, c0, c1), V("u%d" % (t - 1), c0, c1), A.add)

    def add_dma(t, c0, c1):
        o, i = V("u%d" % t, c0, c1), V("u%d" % (t - 1), c0, c1)
        dma("g", ap(o), ap(i), [i, o], [o], add=True)

    def copy_slots(frm, to, c0, c1, shift=0):
        for k in "cs":
            i, o = V(frm + k, c0, c1), V(to + k, c0 + shift, c1 + shift)
            dma("y", raw(o), raw(i), [i], [o])

    def col(k):
        return V("col", k, k + 1)

    def qlist(t):
        return V("qoff", 8 * t, 8 * t + 8)

    def new_products(t):
        for o in range(O):
            mm_new(2 + o, "wt", 128 * o, t)

    def new_copy(t, q, o):
        cp(q, V("yp%d" % o, NS[t], NS[t + 1]), V("ps%d" % (2 + o), 32, 128))

    def y_gather(q, t, *js):
        for o, e in [divmod(j, 2) for j in js]:
            cp(q, V("yb%d" % t, P * o + e, P * o + P, 2), (V("yp%d" % o, 0, NS[t + 1]), V("tab%d" % (t + 1), FY + 8 * e, FY + 8 * e + 8)))

    def y_store(t, o0, o1):
        i = V("yb%d" % t, P * o0, P * o1)
        dma("y", T.y[:, P * (O * t + o0):P * (O * t + o1)], ap(i), [i], [])

    H128, Q2, I1 = V("ct", 0, 1), V("ct", 32, 33), V("ct", 64, 65)
    dma("s", T.qb[:, 0:16], T.qt[:, 0:16], [], [V("qb", 0, 16)])
    for h in range(2):
        dma("y", T.cb[:, 512 * h:512 * h + 512], T.c[:, 512 * h:512 * h + 512], [], [V("cb", 512 * h, 512 * h + 512)])
    for o in range(O):
        dma("y", T.wb[:, 512 * o:512 * o + 512], T.w[:, 512 * o:512 * o + 512], [V("cb", 0, 4 * P)], [V("wb", 512 * o, 512 * o + 512)])
    iota(V("b8", 0, 8), [[1, 2], [0, 4]])
    iota(V("x4", 0, 32), [[0, 8], [4, 4]])
    iota(V("ci", 0, 32), [[128, 2], [0, 16]])
    iota(V("ci", 32, 64), [[0, 2], [2, 16]])
    iota(V("ci", 64, 96), [[1, 32]])
    iota(col(C_P), [[0, 1]], 0, 1)
    iota(V("pr", 0, 128), [[1, 2], [32, 4], [2, 16]])
    fill(V("qb", 16, 512), 0.0)
    fill(qlist(0), 0)
    for s in range(2):
        fill(V("srow%d" % s, 0, 64), 0.0)
    fill(V("cz", 64, 160), 0.0)
    fill(V("cw", 0, 272), -2000.0)
    tr(V("ct", 0, 96), V("ci", 0, 96))
    fill(V("win0", 0, 288), 0.0)
    fill(col(C_E), TINY)
    ts(col(C_A), col(C_P), I1, A.subtract)
    ts(col(C_N), H128, -1.0, A.mult, 128.0, A.add)
    ts(col(C_M), Q2, 16.0, A.is_lt)
    ts(col(C_X), Q2, col(C_A), A.add)
    ts(col(C_W), col(C_N), 1.0 / 128, A.mult, WIN, A.max)
    iota(V("cz", 96, 112), [[1, 8], [9, 2]])
    iota(V("cz", 112, 128), [[1, 8], [-8, 2]], 8)
    iota(V("r3", 0, 32), [[1, 2], [2, 16]])
    iota(V("cw", 16, 16 + K), [[1, K]])
    for j, (b, x, y) in enumerate(((0, 16, 64), (48, -16, -32), (0, 64, 16), (32, -32, 16))):
        for i in range(2):
            act(V("cz", 16 * j + 8 * i, 16 * j + 8 * i + 8), V("b8", 0, 8), AF.Identity, float(b + x * i), float(y))
    cp("s", V("cz", 64, 68), V("cz", 32, 48, 4))
    cp("s", V("cz", 68, 70), V("cz", 32, 48, 8))
    cp("s", V("cz", 84, 86), V("cz", 16, 24, 4))
    for a in range(4):
        for e in range(2):
            x, p = e ^ (a in (1, 2)), 32 * a
            act(V("cz", 160 + e, 192, 2, p, p + 32), V("x4", x, 32, 2, p, p + 32), AF.Identity, 12.0 * (a // 2), 1.0 - 2 * (a // 2))

    ts(V("tab0", FL, FL + 8), V("pr", 0, 128, 16), Q2, A.add, H128, A.add)
    ts(V("tab0", FL + 8, FL + 16), V("pr", 0, 128, 16), Q2, A.add, col(C_N), A.add)
    for h in range(2):
        ts(V("tab0", UL + h, UL + 4, 2), V("pr", 0, 128, 64), col(C_X), A.add, 128.0 * h, A.add)
    ts(V("mm", 0, 128), V("pr", 0, 128), col(C_X), A.is_gt, WIN, A.max)

    quantize("q", 0, "qb")
    for t in (1, 2):
        fill(qlist(t), t)
    pick_codes("qr", 0, "q", 128, qlist(0))
    for t in range(2):
        pick_scales("qr", 128 * t, "q", 128, qlist(t))
    send_codes(PART[2], "qa", 0, "q", 3, 2)

    quantize("w0", 0, "cb")
    mm(0, "qr", 0, "w0", 0, 128)
    act(V("l0", 0, 128), V("ps0", 0, 128), AF.Abs, col(C_E))
    fill(qlist(3), 3)
    quantize("w0", 128, "cb")
    mm(1, "qr", 0, "w0", 128, 128)
    act(V("l0", 128, 256), V("ps1", 0, 128), AF.Abs, col(C_E))
    for t in (1, 2):
        pick_codes("qr", 128 * t, "q", 128, qlist(t))
    mm(5, "qr", 128, "w0", 0, P)
    copy_slots("w0", "w2", 0, P)
    for u in (1, 2, 3):
        iota(V("win%d" % u, 0, 128), [[0, 128]])
    iota(V("zz", 0, 32), [[0, 32]])

    for t in range(R):
        n, tab, nt = NS[t], "tab%d" % t, "tab%d" % (t + 1)
        lw, wn, ls = V("l%d" % t, 0, n), "win%d" % t, "lst%d" % t
        sr, sn = "srow%d" % (t % 2), "srow%d" % ((t + 1) % 2)
        pp = "pb" if t < 2 else "pf"
        off = V("kk", P - 2, P)
        alst = V("alst", 0, 6)
        cp("s", V("u64", 0, 64), (lw, V(tab, UL, UL + 4)))
        cp("s", V("rw", 0, 128), (lw, V(tab, FL + 8, FL + 16)))
        tt(V("rr", 0, 128), (lw, V(tab, FL, FL + 8)), V("mm", 0, 128), A.mult)
        tr(V("t4", 0, 64), V("u64", 0, 64))
        if t == 0:
            for h in range(2):
                square("u0", 128 * h, 128 * h + 128, h, 0)
            square("u1", 0, P, 5, 0)
            for u in (2, 3):
                pick_scales("qr", 128 * u, "q", 128, qlist(u))
            mm(6, "qr", 256, "w0", 0, P)
            square("u2", 0, P, 6, 0)
            for h in range(2):
                for e in range(2):
                    act(V("cz", 128 + 16 * h + e, 134 + 16 * h, 2), V("cz", 96 + 16 * h + e, 102 + 16 * h, 2), AF.Identity, -5.0 * (e != h))
            for c in (0, 16 + K, 16 + 2 * K):
                w = min(16 + K, 272 - c) if c == 0 else min(K, 272 - c)
                act(V("rk", c, c + w), V("cw", min(c, 16), min(c, 16) + w), AF.Identity, float(max(c - 16, 0)))
            ts(V("g1", 0, 32), V("r3", 0, 32), H128, A.add, col(C_A), A.add)
            tr(V("ctr", 96, 128), V("cz", 96, 128))
        if t == 1:
            lift(2, 0, 80)
        if t == 2:
            pick_codes("w2", NS[1], "h", P, V("alst", 0, 4))
            cp("s", V("xs", NS[1], n), (V("hx", 0, P), alst))
            pick_scales("w2", NS[1], "h", P, V("alst", 0, 4))
            pick_scales("w2", NS[1] + 64, "h", P, V("alst", 4, 6))

        def beside():
            new_products(t - 1)
            if t < 3:
                mm_new(1, "qr", 256, t - 1)
            if t == 1:
                mm(0, "qr", 384, "w2", 0, n)
            if t == 2:
                mm_new(0, "qr", 384, 1)
            for o in range(O):
                new_copy(t - 1, "s", o)
            if t < 3:
                square("u2", NS[t - 1], n, 1, 32)
                square("u3", NS[1] * (t - 1), n, 0, 32 * (t - 1))
            if t == 1:
                pick_scales("qx", 0, "qa", 2, qlist(4))
            y_gather("s", t - 1, *range((5, 3, 4)[t - 1]))
        if t == 3:
            y_gather("s", 1, 5)
            gate("y", left)
            y_store(1, 0, O)
        if t in (1, 3):
            beside()
        if t == 3:
            y_store(2, 0, 1)
        for e in range(2):
            ts(V("c%d" % e, 0, 128), V("rr", 0, 128), V("t4", 32 * e, 32 * e + 1), A.is_lt)
        for e in range(2):
            ts(V("c%d" % e, 128, 256), V("rw", 0, 128), col(C_W), A.mult, V("t4", 32 * e, 32 * e + 1), A.is_lt)
        if t == 0:
            ts(V(sr, 16, 48), V("g1", 0, 32), col(C_M), A.mult, EPS, A.max)
        if t == 2:
            tt(V("pay", 0, 32), (V("xs", 0, n), V(tab, PL, PL + 2)), V(sr, 16, 48), A.max)
        for e in range(2):
            a, b, o = V("c%d" % e, 0, 128), V("c%d" % e, 128, 256), V("kk", e, P, 2)
            do("v", lambda: g.vector.tensor_tensor_scan(ap(o), ap(a), ap(b), float(e + 15), A.add, A.add), [a, b], [o])
        if t == 0:
            cp("v", V("co", 4, 5), V("ctr", 96, 97))
        if t == 1:
            lift(2, 80, 160)
        if t == 2:
            pick_codes("w2", NS[1] + 64, "h", P, V("alst", 4, 6))
            copy_slots("w2", "w3", NS[1], n)
            beside()
        cp("v", (V(wn, 0, 272), off), V("pay", 0, 32) if t in (1, 2) else V(sr, 16, 48))
        ts(V("g1", 0, 32), (V("cw", 0, 272), off), float(n), A.add, col(C_M), A.mult)
        k = P if t == 0 else K
        tr(V(pp, 0, k), V(wn, 16, 16 + k))
        tr(V(pp, k, 2 * k + 32), V(wn, 0, 32 + k))
        tt(V(sn, 16, 48), V("g1", 0, 32), V(sr, 16, 48), A.max)
        st = 8 if t == 2 else 16
        m = (2 * k + 32) // st
        tt(V("sa", 0, m, 1, 0, 64), V(pp, 0, m * st, st, 0, 64), V(pp, 0, m * st, st, 64, 128), A.add)
        tr(V("gt", 0, 32), V(sn, 16, 48))
        for p in (0, 32):
            tt(V("sb", 0, m, 1, p, p + 32), V("sa", 0, m, 1, 0, 32), V("sa", 0, m, 1, 32, 64), A.add)
        tr(V("gt", 32, 96), V(sn, 0, 64))
        if t == 2:
            for p in (0, 64):
                tt(V("xo", 0, 3, 1, p, p + 64), V("sb", 1, 12, 4, 0, 64), V("sb", 3, 12, 4, 0, 64), A.add)
            send(PART[t], V("xa", 0, 3), V("xo", 0, 3))
        s2 = 32 // st
        for p in (0, 64):
            tt(V("z7", 0, m // s2, 1, p, p + 64), V("sb", 0, m, s2, 0, 64), V("sb", s2 // 2, m, s2, 0, 64), A.add)
        if t == 0:
            quantize("wt", 0, "wb")
        elif t < 3:
            lift(t + 1, 160 * (t == 1), 160 * (t == 1) + 96)
        cp("v", V(ls, 0, 16), (V("z7", 0, m // s2), V("co", 6, 7) if t else V("co", 4, 5)))
        if t == 0:
            quantize("wt", 128, "wb")
        if t == 2:
            lift(3, 96, 192)
        if t == 1:
            left = send(PART[t], alst, V(ls, 0, 6))
        else:
            pick_codes("out%d" % t, 0, "w%d" % t, n, V(ls, 0, 6))
            pick_scales("out%d" % t, 0, "w%d" % t, n, V(ls, 0, 6))
            left = send_codes(PART[t], *landing(t), "out%d" % t, 0, K)
        if t == 0:
            pick_codes("out0", K, "w0", n, V(ls, 6, 16))
            pick_scales("out0", K, "w0", n, V(ls, 6, 16))
            send_codes(PART[1], "h", K, "out0", K, P - K)
            send_codes(PART[0] ^ PART[1], "h", 0, "out0", 0, K)

        if t == 3:
            y_gather("s", 2, 4)
            y_gather("v", 2, 5)
            y_store(2, 1, O)
        for p in (0, 64):
            cp("s", V("gt", 8, 96, 16, p, p + 64), V("gt", 0, 96, 16, 64 - p, 128 - p))
        for p in range(0, 128, 32):
            cp("s", V("gt", 4, 96, 8, p, p + 32), V("gt", 0, 96, 8, p ^ 32, (p ^ 32) + 32))
        if t == 0:
            cp("s", V("pay", 0, 32), (V("rk", 0, 272), off))
            quantize("wt", 256, "wb")
            for o in range(O):
                mm(5 + o, "wt", 128 * o, "w0", 0, P)
                cp("s", V("yp%d" % o, 0, P), V("ps%d" % (5 + o), 0, P))
            tr(V("ctr", 0, 96), V("cz", 0, 96))
            tr(V("ctr", 128, 192), V("cz", 128, 192))
            add(1, 0, P)
            ts(V("co", 0, 2), V("ctr", 0, 64, 32), V("ctr", 160, 161), A.add)
            cp("v", V("co", 2, 7, 4), V("ctr", 64, 129, 64))
            lift(1, 0, P)
        if t == 1:
            pick_codes("qx", 0, "qa", 2, qlist(4))
            add(2, NS[0], NS[1])
        if t == 2:
            add(3, P, n)
        cp("v", V(nt, 0, 48), (V("gt", 0, 96), V("co", 0, 3)))
        if t == 0:
            ts(qlist(4), qlist(0), col(C_M), A.add)
            add(2, 0, P)
            pick_codes("qr", 384, "q", 128, qlist(3))
            mm_new(1, "qr", 128, 0)
            square("u1", n, n + K, 1, 32)
            lift(1, n, n + K)
        if t == 1:
            need("y", [V(ls, 0, 6)], [])
            copy_slots("w2", "w3", 0, n)
            mm(1, "qr", 256, "h", K, P - K)
            mm(0, "qx", 0, "w2", 0, n)
            mm(2, "qr", 256, "h", 0, 128)
            mm(5, "qx", 0, "h", 0, P)
            square("hq", K, P, 1, 0)
            square("xs", 0, n, 0, 0)
            square("hq", 0, K, 2, 0)
            square("hx", 0, P, 5, 0)
            lift(2, P, NS[1])
            y_gather("v", 0, 5)
            y_store(0, 0, O)
            add(3, 0, P)
            ts(V("l2", n, n + K), (V("hq", 0, P), alst), EPS, A.max)
        if t == 2:
            y_gather("s", 1, 3, 4)
            lift(3, 192, n)
            for j in range(2):
                ts(V("bc", 32 * j, 32 * j + 32), V("zz", 0, 32), V("xa", j, j + 1), A.add)
            act(V("bc", 64, K), V("zz", 0, 32), AF.Identity, V("xa", 2, 3))
            tr(V("l3", n, n + K), V("bc", 0, K))
    new_products(3)
    new_copy(3, "v", 0)
    new_copy(3, "s", 1)
    new_copy(3, "v", 2)
    for o in range(O):
        y_gather("s", 3, 2 * o + 1)
        y_gather("v", 3, 2 * o)
        y_store(3, o, o + 1)

    for sem in count:
        gate("g", sem)
